import numpy as np, ml_dtypes
CORES = [6,15,38,47]
N = 4
BF = ml_dtypes.bfloat16
def gentries(a):
    return np.ascontiguousarray(a.reshape(8, 16, -1).transpose(0, 2, 1)).reshape(8, -1)
def gtable(e):
    e = np.asarray(e); return np.ascontiguousarray(e.reshape(8, -1, 16).transpose(0, 2, 1)).reshape(128, -1).astype(np.int32)
V, D, M, R = 2048, 4, 128, 3
def joined(x):
    return np.stack([gentries(x[r]).reshape(8, D, V) for r in range(N)], 2).reshape(8, D, N * V)
def pack(p, a, w):
    pin, inc = [np.stack([gtable(x.reshape(8, D, N, V)[:, :, r].reshape(8, D * V)) for r in range(N)]) for x in (p, np.argsort(p, -1))]
    return {"part": np.ascontiguousarray(a.transpose(1, 0, 2)).astype(np.int32), "pin": pin, "inc": inc, "w": np.ascontiguousarray(w).astype(np.int32)}
def mix(rng, p, share):
    p = np.array(p); s = np.flatnonzero(rng.random(p.size) < share); p[s] = rng.permutation(p[s]); return p
def clusters(rng, noise):
    p = np.zeros((8, D, N * V), np.int64); h = rng.integers(0, 16, (8, N * V))
    for g in range(8):
        e = np.argsort(rng.permutation(h[g]), kind="stable")
        for i in range(D):
            p[g, i, e] = np.lexsort((rng.random(N * V), h[g])); p[g, i] = mix(rng, p[g, i], noise[g])
    return p, h
def spoil(rng, h, share):
    return np.where(rng.random((8, N, V)) < share, rng.integers(0, 16, (8, N, V)), h.reshape(8, N, V))
def setup_inputs(rng):
    p, h = clusters(rng, rng.random(8) * 0.15)
    return pack(p, spoil(rng, h, rng.random((8, N, 1)) * 0.3), rng.integers(0, 16, (N, 8, V)))
def setup_inputs_ties(rng):
    p = np.stack([np.stack([rng.permutation(N * V) for i in range(D)]) for g in range(8)])
    w = rng.integers(1, 16, (1, 8, 1)) * np.where(np.arange(8)[None, :, None] & 1, rng.integers(0, 2, (N, 8, V)), 1)
    return pack(p, rng.integers(0, 16, (8, N, V)), w)
def setup_inputs_cap(rng):
    n = rng.random(8) * 0.15; n[:3] = 0; p, h = clusters(rng, n); a = spoil(rng, h, rng.random((8, N, 1)) * 0.3)
    w = rng.integers(0, 16, (N, 8, V)); w[:, :3] = np.maximum(w[:, :3], 1); inv = np.argsort(p, -1)
    for g in range(3):
        m = np.array(h[g]); busy = np.zeros(N * V, bool); want = np.roll(np.array([M, M + 1, M - 1, 0, M, 1, M + 1, M // 2])[:N], g)
        for r in range(N):
            left = int(want[r])
            for v in rng.permutation(V // 2) * 2 + (r * V + (g == 2)):
                if left == 0: break
                e = inv[g, :, v]
                if busy[e].any() or len(set(e.tolist())) < D: continue
                busy[e] = True; m[v] = (h[g, v] + rng.integers(1, 16)) & 15; left -= 1
        a[g] = m.reshape(N, V)
    return pack(p, a, w)
def setup_inputs_twins(rng):
    p = np.zeros((8, D, N * V), np.int64); j = np.arange(N * V); a = np.zeros((8, N, V), np.int64)
    for g in range(8):
        b = j if g == 0 else (j + V) % (N * V) if g == 1 else rng.permutation(N * V); s = 0.3 + 0.5 * rng.random()
        for i in range(D): p[g, i] = b if i == 0 else mix(rng, b, s)
        u = rng.permutation(16)[:rng.integers(2, 17)]; a[g] = u[rng.integers(0, u.size, (N, V))]
    return pack(p, a, rng.integers(0, 16, (N, 8, V)))
def setup_inputs_spread(rng):
    p, h = clusters(rng, rng.random(8)); k = 2.0 ** rng.integers(0, 5, (8, N, 1))
    q = np.minimum((16 * rng.random((8, N, V)) ** k).astype(np.int64), 15)
    a = np.where(rng.random((8, N, V)) < rng.random((8, N, 1)), q, h.reshape(8, N, V))
    w = np.where(rng.random((N, 8, V)) < rng.random((N, 8, 1)), rng.choice(np.array([0, 15]), (N, 8, V)), rng.integers(0, 16, (N, 8, V)))
    return pack(p, a, w)
def check_inputs(d):
    bad = [n for n, top in (("part", 16), ("pin", N * V), ("inc", N * V), ("w", 16)) if np.min(d[n]) < 0 or np.max(d[n]) >= top]
    if not bad:
        p, q, j = joined(d["pin"]), joined(d["inc"]), np.arange(N * V)
        if (np.sort(p, -1) != j).any(): bad.append("every vertex once at each position of pin")
        elif (np.take_along_axis(q, p, -1) != j).any(): bad.append("inc is the inverse of pin")
    return bad
def counts(a, p):
    return np.sum(a[p][None] == np.arange(16)[:, None, None], 1)
def reference(part, pin, inc, w):
    a = np.array(part.transpose(1, 0, 2)).reshape(8, N * V).astype(np.int64); wt = np.array(w.transpose(1, 0, 2)).reshape(8, N * V).astype(np.int64)
    p, e, j = joined(pin), joined(inc), np.arange(N * V); cut = np.zeros(8, np.int64)
    for g in range(8):
        for t in range(R):
            c = counts(a[g], p[g]); one = wt[g] * (c == 1); none = wt[g] * (c == 0)
            gain = np.sum(one[np.broadcast_to(a[g], (D, N * V)), e[g]], 0) - np.sum(none[:, e[g]], 1)
            gain[a[g], j] = -1000000
            best = np.argmax(gain, 0)
            can = ((gain[best, j] > 0) & (((j % V) + t) % 2 == 0)).reshape(N, V)
            go = (can & (np.add.accumulate(can.astype(np.int64), 1) <= M)).reshape(-1)
            a[g] = np.where(go, best, a[g])
        cut[g] = np.sum(wt[g] * (np.sum(counts(a[g], p[g]) > 0, 0) - 1))
    return {"newpart": np.ascontiguousarray(a.reshape(8, N, V).transpose(1, 0, 2)).astype(np.float32), "cut": np.repeat(cut.astype(np.float32)[None, :, None], N, 0)}

@@ -1,0 +1,484 @@
+from concourse.bass import DstId, RemoteDMATransfer
+from concourse.mybir import AluOpType as A, ActivationFunctionType as F
+
+BIG = 1.5 * 2.0 ** 33
+KQ = 32
+NA = KQ // 4
+SCRATCH = {
+    "DY": ("dram", [4, 128, 64], "int32"),
+    "DI": ("dram", [4, 128, 128], "int32"),
+    "DO": ("dram", [4, 128, 32], "float32"),
+    "LO": ("dram", [4, 128, 32], "float32"),
+    "S0": ("psum", [128, 1024], "float32"),
+    "S1": ("psum", [128, 1024], "float32"),
+    "S2": ("psum", [128, 1024], "float32"),
+    "S3": ("psum", [128, 1024], "float32"),
+}
+for _names, _shape, _dt in [
+        ("Y", [4, 64], "int32"), ("Yb Yw Yj", [4, 64], "bfloat16"), ("W", [2048], "bfloat16"),
+        ("S32", [512], "int32"), ("S16 PL IL", [512], "uint16"), ("ILi", [4, 2, 64], "int32"),
+        ("P TT R", [8192], "bfloat16"), ("G", [4096], "bfloat16"),
+        ("KI", [4], "int32"), ("CI", [8], "int32"), ("CF", [16], "float32"), ("J32", [36], "float32"),
+        ("JP JH VAL HM B1 B2 E EI E1 E2", [32], "float32"), ("NE", [4], "float32"),
+        ("BI BSE C ONE IDN TRI SWF OD GD DT0 DT1", [128], "bfloat16"),
+        ("SELI", [32, 128], "bfloat16"), ("SEL", [NA, 128], "bfloat16"), ("SW", [4, 128], "bfloat16"),
+        ("Z", [224], "bfloat16"), ("R1 R2", [32], "bfloat16"), ("MSK", [512], "float32"), ("MA MW", [2], "float32"),
+        ("SC", [2, 512], "float32"), ("KY KO KB", [2, 32], "int32"), ("KR DL GO", [2, 32], "float32"),
+        ("CP", [4, 32], "bfloat16"), ("O", [256], "float32"), ("ACC", [8], "float32"), ("CL", [4, 4], "float32")]:
+    for _n in _names.split():
+        SCRATCH[_n] = ("sbuf", [128] + _shape, _dt)
+SEMAPHORES = (["ev", "ea", "et", "eg", "dy", "dyo", "dp", "di", "dio", "do", "dn", "dc", "ca", "sent"]
+              + ["%s%d" % (n, q) for n in ("ya", "pa", "ia", "oa", "dw") for q in range(4)])
+
+
+def rank_program(g, core, T, topo):
+    me = T.rank_of(core)
+    if me is None:
+        return
+    cores = T.cores
+    n = len(cores)
+    Q = {"v": g.vector, "a": g.scalar, "t": g.tensor, "g": g, "s": g.sync}
+    own = {"v": "ev", "a": "ea", "t": "et", "g": "eg"}
+    cnt = dict((s, 0) for s in SEMAPHORES)
+    clock = dict((q, {}) for q in Q)
+    waited = dict((s, 0) for s in SEMAPHORES)
+    wr, rd = {}, {}
+
+    def need(q, tok):
+        s, v, ck, src = tok
+        if src == "t" and q == "t":
+            return
+        if v is None:
+            v = cnt[s]
+        if clock[q].get(s, 0) < v:
+            Q[q].wait_ge(T.sem[s], v)
+            waited[s] = max(waited[s], v)
+            clock[q][s] = v
+        for k in ck:
+            if clock[q].get(k, 0) < ck[k]:
+                clock[q][k] = ck[k]
+
+    def deps(q, reads, writes):
+        toks = [wr[k] for k in list(reads) + list(writes) if k in wr]
+        for k in writes:
+            toks += rd.get(k, [])
+        toks.sort(key=lambda t: -(t[1] if t[1] is not None else cnt[t[0]]))
+        for t in toks:
+            need(q, t)
+
+    def mark(tok, reads, writes):
+        for k in writes:
+            wr[k] = tok
+            rd[k] = []
+        for k in reads:
+            rd.setdefault(k, []).append(tok)
+
+    def op(q, call, reads, writes):
+        deps(q, reads, writes)
+        s = own[q]
+        cnt[s] += 1
+        call().then_inc(T.sem[s], 1)
+        mark((s, cnt[s], dict(clock[q]), q), reads, writes)
+
+    def dma(q, out, in_, s, reads, writes):
+        deps(q, reads, writes)
+        cnt[s] += 16
+        Q[q].dma_start(out, in_).then_inc(T.sem[s], 16)
+        mark((s, None, dict(clock[q]), "dma"), reads, writes)
+
+    def lands(key, s, v):
+        cnt[s] += v
+        wr[key] = (s, None, {}, "far")
+
+    V, S, PE = g.vector, g.scalar, g.tensor
+
+    def ts(out, in0, s1, s2, o0, o1, reads, writes):
+        if o1 is None:
+            op("v", lambda: V.tensor_scalar(out, in0, s1, None, o0), reads, writes)
+        else:
+            op("v", lambda: V.tensor_scalar(out, in0, s1, s2, o0, o1), reads, writes)
+
+    def tt(out, a, b, o, reads, writes):
+        op("v", lambda: V.tensor_tensor(out, a, b, o), reads, writes)
+
+    def cp(q, out, in_, reads, writes):
+        if q == "v":
+            op("v", lambda: V.tensor_copy(out, in_), reads, writes)
+        else:
+            op("a", lambda: S.activation(out, in_, F.Copy), reads, writes)
+
+    def mm(out, l, r, st, sp, reads, writes):
+        op("t", lambda: PE.matmul(out, l, r, st, sp), reads, writes)
+
+    def ms(ap, c, writes):
+        op("v", lambda: V.memset(ap, c), [], writes)
+
+    def io(out, pat, base, cm, writes, flag=True):
+        if flag:
+            op("g", lambda: g.iota(out, pat, base, cm, allow_small_or_imprecise_dtypes=True), [], writes + ["POOL"])
+        else:
+            op("g", lambda: g.iota(out, pat, base, cm), [], writes + ["POOL"])
+
+    def af(out, in_, pat, cmp, fill, base, cm, reads, writes):
+        op("g", lambda: g.affine_select(out, in_, pat, cmp, fill, base, cm), reads, writes + ["POOL"])
+
+    def hops(a, b):
+        ca, cb = topo.chip(cores[a]), topo.chip(cores[b])
+        return 0 if ca == cb else 1 if topo.mates(ca, cb) else 2 if topo.same_plane(ca, cb) else 3
+
+    def peers(a):
+        return sorted([b for b in range(n) if b != a], key=lambda b: (hops(a, b), b))
+
+    def share(a, turn):
+        ps = peers(a)
+        en = [e for e in topo.engines(cores[a], cores[ps[0]]) if all(e in topo.engines(cores[a], cores[b]) for b in ps)]
+        k = len(en) // 4
+        cuts = [en[:2 * k], en[2 * k:3 * k], en[3 * k:4 * k]]
+        return dict((b, cuts[(j + turn) % 3]) for j, b in enumerate(ps))
+
+    def bits(en):
+        return sum(1 << e for e in en)
+
+    def dst(b):
+        rid, pid, _e = topo.addr(cores[b])
+        return DstId(rid=rid, pnc=pid)
+
+    def fused(turn, name, src, land, reads):
+        deps("g", reads, [])
+        sh = share(me, turn)
+        g.remote_dma_fused([RemoteDMATransfer(dst_ids=[dst(b)], dma_engine_mask=bits(sh[b]),
+                                              remote_sem=T.sem["%s%d" % (name, me)], src=src(b), dst=land)
+                            for b in others], local_sem=T.sem.sent)
+        cnt["sent"] += sum(len(sh[b]) for b in others)
+
+    others = peers(me)
+    order = [me] + others
+    for b in others:
+        lands(("Y", b), "ya%d" % b, len(topo.engines(cores[b], core)))
+        lands(("PL", b), "pa%d" % b, len(share(b, 0)[me]))
+        lands(("ILi", b), "ia%d" % b, len(share(b, 1)[me]))
+        lands(("LO", b), "oa%d" % b, len(share(b, 1)[me]))
+        lands("CLfar", "ca", sum(len(x) for x in share(b, 0).values()))
+
+    dma("s", T.DY[:, 0:64, :], T.part[:], "dy", [], [("DY", 0)])
+    dma("a", T.DY[:, 64:128, :], T.w[:], "dy", [], [("DY", 1)])
+    DYK = [("DY", 0), ("DY", 1)]
+    dma("s", T.Y[0:64, me, :], T.part[2 * me:2 * me + 2, :], "dyo", [], [("Y", me)])
+    dma("a", T.Y[64:128, me, :], T.w[2 * me:2 * me + 2, :], "dyo", [], ["Yown"])
+    for r in range(4):
+        for i in range(4):
+            dma("s" if i < 2 else "a", T.S32[32 * i:32 * i + 32, 128 * r:128 * r + 128],
+                T.pin[32 * r:32 * r + 32, 128 * i:128 * i + 128], "dp", [], [("S32", r, i)])
+    S32K = [("S32", r, i) for r in range(4) for i in range(4)]
+
+    io(T.KI[:, 0:1], [[0, 1]], 0, 1, ["KI"], False)
+    io(T.J32[:], [[1, 36]], 0, 0, ["J32"])
+    io(T.JH[:], [[1, 2], [0, 16]], 0, 0, ["JH"])
+    io(T.JP[:], [[0, 2], [1, 16]], 0, 0, ["JP"])
+    deps("g", DYK, [])
+    for b in others:
+        rid, pid, _e = topo.addr(cores[b])
+        g.remote_dma(T.Y[:, me, :], T.DY[b], T.sem["ya%d" % me], T.sem.sent, pid, rid, topo.mask(core, cores[b]))
+        cnt["sent"] += len(topo.engines(core, cores[b]))
+
+    for j, (sh_, an) in enumerate([(0, 31), (5, 3), (0, 15), (1, 1), (0, 1), (2, NA - 1), (4, 1)]):
+        ts(T.CI[:, j:j + 1], T.KI[:, 0:1], sh_, an, A.logical_shift_right, A.bitwise_and, ["KI"], [("CI", j)])
+    ms(T.Yb[64:128], 1.0, ["Yb1"])
+    cp("v", T.CF[:, 0:7], T.CI[:, 0:7], [("CI", j) for j in range(7)], ["CF"])
+
+    def col(j):
+        return T.CF[:, j:j + 1]
+
+    def scaled(j, out, in_, c, reads, writes):
+        if j % 4 == 3:
+            op("a", lambda: S.activation(out, in_, F.Identity, scale=c), reads, writes)
+        else:
+            ts(out, in_, c, None, A.mult, None, reads, writes)
+    ts(col(14), col(1), 2.0, None, A.is_equal, None, ["CF"], ["c14"])
+    ts(col(15), col(1), 2.0, -2.0, A.is_equal, A.mult, ["CF"], ["c15"])
+    ts(T.EI[:], T.J32[:, 0:32], col(0), None, A.is_equal, None, ["J32", "CF"], ["EI"])
+    ts(T.B1[:], T.JH[:], col(1), 2.0, A.is_equal, A.mult, ["JH", "CF"], ["B1"])
+    ts(T.B2[:], T.JP[:], col(15), col(14), A.mult, A.add, ["JP", "c14", "c15"], ["B2"])
+    for i in range(4):
+        tt(T.BI[:, 32 * i:32 * i + 32], T.B1[:], T.B2[:], A.add, ["B1", "B2"], [("BI", i)])
+    for a in range(32):
+        scaled(a, T.SELI[:, a, :], T.BI[:], T.EI[:, a:a + 1], [("BI", i) for i in range(4)] + ["EI"], [("SELI", a)])
+    SELK = [("SEL", a) for a in range(NA)]
+    CK = [("C", i) for i in range(4)]
+
+    def pins():
+        cp("v", T.S16[:], T.S32[:], S32K, ["S16"])
+        fused(0, "pa", lambda b: T.S16[:, 128 * b:128 * b + 128], T.PL[:, 128 * me:128 * me + 128], ["S16"])
+
+    def more():
+        cp("v", T.PL[:, 128 * me:128 * me + 128], T.S16[:, 128 * me:128 * me + 128], ["S16"], [("PL", me)])
+        ms(T.Z[:], 0.0, ["Z"])
+        ts(col(11), col(2), 0.0, None, A.is_equal, None, ["CF"], ["c11"])
+        ts(col(8), col(4), -2.0, None, A.mult, None, ["CF"], ["c8"])
+        ts(col(9), col(4), -1.0, 2.0, A.mult, A.add, ["CF"], ["c9"])
+        ts(col(12), col(11), 16.0, col(0), A.mult, A.add, ["c11", "CF"], ["c12"])
+        ts(col(13), col(11), -16.0, 8.0, A.mult, A.add, ["c11"], ["c13"])
+        ts(T.E1[:], T.EI[:], -8.0, None, A.mult, None, ["EI"], ["E1"])
+        ts(T.NE[:], T.J32[:, 0:4], col(1), None, A.not_equal, None, ["J32", "CF"], ["NE"])
+        ts(T.E2[:], T.J32[:, 1:33], col(12), col(13), A.is_equal, A.mult, ["J32", "c12", "c13"], ["E2"])
+        ts(T.HM[:], T.JH[:], col(3), None, A.is_equal, None, ["JH", "CF"], ["HM"])
+        tt(T.Z[:, 96:128], T.E1[:], T.E2[:], A.add, ["E1", "E2"], ["Z"])
+        ts(T.VAL[:], T.JP[:], col(8), col(9), A.mult, A.add, ["JP", "c8", "c9"], ["VAL"])
+        for i in range(4):
+            scaled(3, T.C[:, 32 * i:32 * i + 32], T.Z[:, 96:128], T.NE[:, i:i + 1], ["Z", "NE"], [("C", i)])
+        ts(T.E[:, 0:NA], T.J32[:, 0:NA], col(5), None, A.is_equal, None, ["J32", "CF"], ["E"])
+        for i in range(4):
+            tt(T.BSE[:, 32 * i:32 * i + 32], T.VAL[:], T.HM[:], A.mult, ["VAL", "HM"], [("BSE", i)])
+        ts(T.R1[:], T.EI[:], 1024.0, None, A.mult, None, ["EI"], ["R1"])
+        ts(T.MA[:], T.J32[:, 0:2], col(6), -1.0, A.is_equal, A.mult, ["J32", "CF"], ["MA"])
+        ts(T.MW[:], T.J32[:, 2:4], col(1), 15.0, A.is_equal, A.mult, ["J32", "CF"], ["MW"])
+        for a in range(NA):
+            scaled(3, T.SEL[:, a, :], T.BSE[:], T.E[:, a:a + 1], [("BSE", i) for i in range(4)] + ["E"], [("SEL", a)])
+        ms(T.CL[:, me, :], 0.0, ["CLown"])
+
+    SL = [T.S0, T.S1, T.S2, T.S3]
+
+    def banks(k):
+        return [("B", 2 * k), ("B", 2 * k + 1)]
+
+    def sign(q, out, k, y, writes):
+        src, bk = (SL[k][:], banks(k)) if y is None else (SL[k][:, 512 * y:512 * y + 512], [("B", 2 * k + y)])
+        if q == "v":
+            ts(out, src, -1.0, 1.0, A.max, A.min, [], writes + bk)
+        else:
+            op("a", lambda: S.activation(out, src, F.Sign), [], writes + bk)
+
+    PK = [("P", q, x) for q in range(4) for x in range(4)]
+    RK = [("R", q, x) for q in range(4) for x in range(2)]
+
+    def take(j):
+        q = order[j]
+        cp("v", T.Yb[0:64, q, :], T.Y[0:64, q, :], [("Y", q)], [("Yb", q)])
+        for y in range(4):
+            k = 2 * (j % 2) + y // 2
+            for al in range(8 * y, 8 * y + 8):
+                c0 = 64 * (al % 16)
+                mm(SL[k][:, c0:c0 + 64], T.SELI[0:96, al, :], T.Yb[0:96, q, :], True, True,
+                   [("SELI", al), ("Yb", q), "Yb1"], [("B", 2 * k + y % 2)])
+        cp("v", T.Yw[64:128, q, :], T.Y[64:128, q, :], [("Y", q), "Yown"], [("Yw", q)])
+        for h in range(2):
+            dma("s", T.W[2 * q + h:2 * q + h + 1, :], T.Yw[64 + 32 * h:96 + 32 * h, q, :], "dw%d" % q, [("Yw", q)], [("W", q, h)])
+
+    def put(j):
+        q = order[j]
+        for y in range(4):
+            sign("av"[y % 2], T.P[:, 2048 * q + 512 * y:2048 * q + 512 * y + 512], 2 * (j % 2) + y // 2, y % 2, [("P", q, y)])
+    take(0); pins(); put(0); more(); take(1); take(2); put(1); take(3); put(2); put(3)
+    WK = [("W", q, h) for q in range(4) for h in range(2)]
+    for i in range(4):
+        for pi in range(2):
+            dma("s", T.DI[:, 32 * i:32 * i + 32, 64 * pi:64 * pi + 64], T.inc[pi::2, 128 * i:128 * i + 128],
+                "di", [], [("DI", i, pi)])
+    DIK = [("DI", i, pi) for i in range(4) for pi in range(2)]
+    dma("s", T.ILi[:, me], T.DI[me], "dio", DIK, [("ILi", me)])
+
+    io(T.ONE[:], [[0, 128]], 1, 0, ["ONE"])
+    for q in order:
+        af(T.SW[0:8, q, :], T.ONE[0:8, :], [[0, 4], [-1, 2], [0, 16]], A.is_equal, 0.0, -2 * q, 1, ["ONE"], [("SW", q)])
+    hp = [[-16, 2], [0, 16]]
+    r2 = [T.R2[32 * j:32 * j + 32, :] for j in range(4)]
+    io(r2[0], [[0, 32]], 1, 0, [("R2", 0)])
+    io(r2[1], [[0, 2], [32, 16]], 512, 0, [("R2", 1)])
+    io(r2[2], [[0, 2], [-16, 16]], -256, 0, [("R2", 2)])
+    io(r2[3], [[0, 2], [16, 16]], 256, 0, [("R2", 3)])
+    af(r2[0], r2[0], hp, A.not_equal, 15.0, 0, 1, [("R2", 0)], [("R2", 0)])
+    af(r2[1], r2[1], hp, A.is_equal, 0.0, 0, 1, [("R2", 1)], [("R2", 1)])
+    af(r2[2], r2[2], [[-1, 32]], A.is_equal, 0.0, 0, 1, [("R2", 2)], [("R2", 2)])
+    af(r2[3], r2[3], [[-1, 32]], A.is_equal, 0.0, -1, 1, [("R2", 3)], [("R2", 3)])
+    af(r2[0], r2[0], hp, A.is_ge, 0.0, 0, 1, [("R2", 0)], [("R2", 0)])
+    last = T.R2[96:128, 15::16]
+    io(last, [[0, 2]], -496, 0, [("R2", 3)])
+    af(r2[0], r2[0], [[16, 2], [0, 16]], A.is_ge, 0.0, 15, -1, [("R2", 0)], [("R2", 0)])
+    af(last, last, [[-16, 2]], A.is_equal, 0.0, 0, 1, [("R2", 3)], [("R2", 3)])
+    R2K = [("R2", j) for j in range(4)]
+    io(T.MSK[:], [[0, 512]], 131072, 0, ["MSK"])
+    fused(1, "ia", lambda b: T.DI[b], T.ILi[:, me], DIK)
+    af(T.MSK[:], T.MSK[:], [[0, 32], [1, 16]], A.is_equal, 0.0, 0, 0, ["MSK"], ["MSK"])
+    io(T.CP[:], [[0, 128]], 0, 0, [("CP", 0), ("CP", 1)])
+    af(T.TRI[:], T.ONE[:], [[1, 128]], A.is_gt, 0.0, 0, -1, ["ONE"], ["TRI"])
+    af(T.TRI[:], T.TRI[:], [[1, 128]], A.not_equal, -512.0, 0, -1, ["TRI"], ["TRI"])
+    io(T.OD[:], [[0, 128]], 1, 0, [("OD", 0), ("OD", 1)])
+    io(T.GD[:], [[0, 128]], 0, 0, [("GD", 0), ("GD", 1)])
+    af(T.IDN[:], T.ONE[:], [[-1, 128]], A.is_equal, 0.0, 0, 1, ["ONE"], ["IDN"])
+    af(T.SWF[0:8, :], T.ONE[0:8, :], [[-1, 8], [0, 16]], A.is_equal, 0.0, 0, 1, ["ONE"], ["SWF"])
+
+    def gather_pin(e, c0, m, key):
+        cp(e, T.TT[:, c0:c0 + m], T.P[:, 0:8192].indirect(T.PL[:, c0 // 16:(c0 + m) // 16]), PK + [("PL", c0 // 2048)], key)
+
+    def lists(pi):
+        cp("v", T.IL[:, 256 * pi:256 * pi + 256], T.ILi[:, :, pi, :], [("ILi", q) for q in range(4)], [("IL", pi)])
+
+    for t in range(3):
+        pi = t % 2
+        DT = T.DT1 if pi else T.DT0
+
+        def g1(j):
+            for x in range(2):
+                q = order[j]
+                gather_pin("va"[x], 2048 * q + 1024 * x, 1024, [("TT", q, 2 * x), ("TT", q, 2 * x + 1)])
+
+        def rec(j):
+            q = order[j]
+            for first in (True, False):
+                for x in range(2):
+                    k = 2 * x + j % 2
+                    for y in range(2):
+                        e0 = 1024 * x + 512 * y
+                        o = SL[k][:, 512 * y:512 * y + 512]
+                        if first:
+                            mm(o, T.SW[0:8, q, :], T.W[0:8, e0:e0 + 512], True, False, WK + [("SW", q)], [("B", 2 * k + y)])
+                        else:
+                            mm(o, T.C[:], T.TT[:, 2048 * q + e0:2048 * q + e0 + 512], False, True,
+                               CK + [("TT", q, 2 * x + y)], [("B", 2 * k + y)])
+
+        def relu(j):
+            q = order[j]
+            for x in range(2):
+                k = 2 * x + j % 2
+                o = T.R[:, 2048 * q + 1024 * x:2048 * q + 1024 * x + 1024]
+                if x == 0:
+                    ts(o, SL[k][:], 0.0, None, A.max, None, [], [("R", q, x)] + banks(k))
+                else:
+                    op("a", lambda: S.activation(o, SL[k][:], F.Relu), [], [("R", q, x)] + banks(k))
+        g1(0); rec(0); g1(1); rec(1); relu(0); g1(2); rec(2); relu(1); g1(3); rec(3); relu(2)
+        if t == 0:
+            lists(0)
+        relu(3)
+
+        def g2(e, u):
+            cp(e, T.G[:, 512 * u:512 * u + 512], T.R[:, 0:8192].indirect(T.IL[:, 256 * pi + 32 * u:256 * pi + 32 * u + 32]),
+               RK + [("IL", pi)], [("G", u)])
+
+        def keys(u):
+            q, hf = u // 2, u // 4
+            for bb in range(2 * (u % 2), 2 * (u % 2) + 2):
+                for xb in range(2):
+                    blk = 4 * xb + bb
+                    c0 = 512 * hf + 32 * (8 * (q % 2) + blk)
+                    o = T.S0[:, c0:c0 + 32]
+                    p0 = 2048 * q + 256 * blk
+                    g0 = 1024 * q + 256 * bb
+                    mm(o, T.P[:, p0 + pi:p0 + 256:2], T.R2[:], True, False, PK + R2K, [("B", hf)])
+                    mm(o, T.G[:, g0 + xb:g0 + 256:2], T.R1[:], False, True, [("G", u), "R1"], [("B", hf)])
+
+        def chain(hf, mid, fill):
+            pb = ("B", 2 + hf)
+            ps = T.S1[:, 512 * hf:512 * hf + 32]
+            op("v", lambda: V.tensor_tensor_scan(T.SC[:, hf, :], T.MSK[:], T.S0[:, 512 * hf:512 * hf + 512], 0.0, A.add, A.min),
+               ["MSK"], [("SC", hf), ("B", hf)])
+            key = T.SC[:, hf, 15::16]
+            ts(T.KR[:, hf, :], key, BIG, -BIG, A.add, A.add, [("SC", hf)], [("KR", hf)])
+            cp("v", T.KY[:, hf, :], key, [("SC", hf)], [("KY", hf)])
+            tt(T.CP[:, 2 * hf:2 * hf + 2, 16:32], T.KR[:, hf, :], key, A.is_gt, [("KR", hf), ("SC", hf)], [("CP", hf)])
+            for s in range(8):
+                mm(ps, T.TRI[:] if s == 0 else T.ONE[:], T.CP[:, 2 * hf:2 * hf + 2, 16 - 2 * s:32 - 2 * s], s == 0, s == 7,
+                   ["TRI", "ONE", ("CP", hf)], [pb])
+            mid()
+            ts(T.KO[:, hf, :], T.KY[:, hf, :], 1, 15, A.logical_shift_right, A.bitwise_and, [("KY", hf)], [("KO", hf)])
+            ts(T.KB[:, hf, :], T.KY[:, hf, :], 5, 15, A.logical_shift_right, A.bitwise_and, [("KY", hf)], [("KB", hf)])
+            cp("v", T.OD[:, 64 * hf:64 * hf + 64:2], T.KO[:, hf, :], [("KO", hf)], [("OD", hf)])
+            tt(T.DL[:, hf, :], T.KB[:, hf, :], T.KO[:, hf, :], A.subtract, [("KB", hf), ("KO", hf)], [("DL", hf)])
+            ts(T.GO[:, hf, :], ps, -384.5, None, A.is_lt, None, [], [("GO", hf), pb])
+            tt(T.GD[:, 64 * hf:64 * hf + 64:2], T.GO[:, hf, :], T.DL[:, hf, :], A.mult, [("GO", hf), ("DL", hf)], [("GD", hf)])
+            fill()
+            pt = T.S1[64 * hf:64 * hf + 64, 512 * hf + 128:512 * hf + 256]
+            mm(pt, T.OD[:, 64 * hf:64 * hf + 64], T.IDN[:], True, False, [("OD", hf), "IDN"], [pb])
+            mm(pt, T.GD[:, 64 * hf:64 * hf + 64], T.IDN[:], False, True, [("GD", hf), "IDN"], [pb])
+            return pt
+
+        def turn(e, hf, pt):
+            cp(e, DT[64 * hf:64 * hf + 64, :], pt, [], [("DT", pi, hf), ("B", 2 + hf)])
+
+        def spread_mm(q, k, y):
+            lo = KQ * (32 * q // KQ)
+            for blk in range(4 * y, 4 * y + 4):
+                mm(SL[k][:, 128 * blk:128 * blk + 128], T.SEL[lo:lo + KQ, (8 * q + blk) % NA, :], DT[lo:lo + KQ, :], True, True,
+                   SELK + [("DT", pi, q // 2)], [("B", 2 * k + y)])
+
+        def spread(e, q, k, y):
+            if y is None:
+                sign(e, T.P[:, 2048 * q + pi:2048 * q + 2048:2], k, None, [("P", q, z) for z in range(4)])
+            else:
+                c0 = 2048 * q + 1024 * y
+                sign(e, T.P[:, c0 + pi:c0 + 1024:2], k, y, [("P", q, 2 * y), ("P", q, 2 * y + 1)])
+
+        g2("v", 0); g2("a", 2); keys(0); keys(2)
+        g2("v", 1); g2("a", 3); keys(1); keys(3)
+        g2("v", 4); g2("a", 5); g2("a", 6); g2("a", 7)
+        keys(4); keys(5)
+        pa = chain(0, lambda: keys(6), lambda: lists(1) if t == 0 else None)
+        keys(7)
+        if t == 0:
+            op("a", lambda: S.activation(T.Yj[64:128], T.Yw[64:128], F.Identity, accum_out=T.ACC[64:128, 4:5]),
+               [("Yw", q) for q in range(4)], ["Yj", ("ACC", 4)])
+        turn("a", 0, pa)
+        if t == 2:
+            cp("a", T.O[:, 1::2], T.DT1[:], [("DT", 1, 0), ("DT", 1, 1)], ["O1"])
+        spread_mm(0, 2, 0); spread_mm(0, 2, 1); spread_mm(1, 3, 0); spread_mm(1, 3, 1)
+        spread("a", 0, 2, 0); spread("a", 0, 2, 1); spread("a", 1, 3, None)
+        pb_ = chain(1, lambda: None, lambda: None)
+        turn("v", 1, pb_)
+        if t == 2:
+            cp("a", T.O[:, 0::2], T.DT0[:], [("DT", 0, 0), ("DT", 0, 1)], ["O0"])
+        for y in range(2):
+            spread_mm(2, 0, y); spread_mm(3, 2, y)
+        for y in range(2):
+            spread("v", 2, 0, y); spread("a", 3, 2, y)
+
+    for h in range(2):
+        dma("s", T.DO[:, 64 * h:64 * h + 64, :], T.O[2 * h::4, :], "do", ["O0", "O1"], [("DO", h)])
+    for h in range(2):
+        dma("s", T.newpart[2 * me + h:2 * me + h + 1, :], T.O[32 * me + 2 * h:32 * me + 32:4, :], "dn", ["O0", "O1"], [])
+    fused(1, "oa", lambda b: T.DO[b], T.LO[me], [("DO", 0), ("DO", 1)])
+    for b in others:
+        dma("s", T.newpart[2 * b:2 * b + 2, :], T.LO[b], "dn", [("LO", b)], [])
+
+    fb = [(T.S1, 0, 2), (T.S1, 512, 3), (T.S3, 0, 6), (T.S3, 512, 7)]
+    cutp = T.S0[0:1, 0:2]
+
+    def g3(e, c, q):
+        gather_pin(e, 2048 * q + 512 * c, 512, [("TT", q, c)])
+
+    def cnt3(c, qs):
+        buf, c0, bk = fb[c]
+        o = buf[:, c0:c0 + 512]
+        mm(o, T.SWF[0:8, :], T.W[0:8, 512 * c:512 * c + 512], True, False, WK + ["SWF"], [("B", bk)])
+        for q in qs:
+            mm(o, T.Z[:, 96 - 32 * q:224 - 32 * q], T.TT[:, 2048 * q + 512 * c:2048 * q + 512 * c + 512], False, q == qs[-1],
+               ["Z", ("TT", q, c)], [("B", bk)])
+
+    def sum3(c):
+        buf, c0, bk = fb[c]
+        op("a", lambda: S.activation(T.G[:, 512 * c:512 * c + 512], buf[:, c0:c0 + 512], F.Relu, accum_out=T.ACC[:, c:c + 1]),
+           [], [("G", c), ("ACC", c), ("B", bk)])
+
+    for c in range(2):
+        g3("v", c, 0); g3("a", c, 2); g3("v", c, 1); g3("a", c, 3)
+        cnt3(c, [0, 2, 1, 3])
+    sum3(0)
+    g3("v", 2, 0); g3("a", 2, 2); g3("v", 2, 1); g3("a", 2, 3)
+    cnt3(2, [0, 1, 2, 3])
+    sum3(1)
+    g3("v", 3, 0); g3("a", 3, 3); g3("v", 3, 1); g3("v", 3, 2)
+    sum3(2)
+    cnt3(3, [0, 3, 1, 2])
+    sum3(3)
+    mm(cutp, T.ACC[64:128, 4:5], T.MW[64:128, :], True, False, [("ACC", 4), "MW"], [("B", 0)])
+    for c in range(4):
+        mm(cutp, T.ACC[:, c:c + 1], T.MA[:], False, c == 3, [("ACC", c), "MA"], [("B", 0)])
+    cp("v", T.CL[0:1, me, 0:2], cutp, [], ["CLown", ("B", 0)])
+    deps("g", ["CLown"], [])
+    en = [e for x in share(me, 0).values() for e in x]
+    g.remote_dma_fused([RemoteDMATransfer(dst_ids=[dst(b) for b in others], dma_engine_mask=bits(en), remote_sem=T.sem.ca,
+                                          srcs=[T.CL[:, me, :]], dsts=[T.CL[:, me, :] for b in others])], local_sem=T.sem.sent)
+    cnt["sent"] += len(en)
+    dma("s", T.cut[:], T.CL[0:1, :, 0:2], "dc", ["CLown", "CLfar"], [])
+
+    for s in SEMAPHORES:
+        if cnt[s] > waited[s]:
+            (g if s in ("sent", "eg") else g.sync).wait_ge(T.sem[s], cnt[s])

@@ -1,33 +1,39 @@
 from concourse.bass import DstId, RemoteDMATransfer
-from concourse.mybir import AluOpType as A, ActivationFunctionType as F
+from concourse.mybir import AluOpType as A, ActivationFunctionType as F, AxisListType as AX
 
-BIG = 1.5 * 2.0 ** 33
-KQ = 32
-NA = KQ // 4
+R2048, R128, R32 = 1.5 * 2.0 ** 34, 1.5 * 2.0 ** 30, 1.5 * 2.0 ** 28
+WIN = 8192 + 512
+SEED = WIN // 16
 SCRATCH = {
     "DY": ("dram", [4, 128, 64], "int32"),
     "DI": ("dram", [4, 128, 128], "int32"),
-    "DO": ("dram", [4, 128, 32], "float32"),
-    "LO": ("dram", [4, 128, 32], "float32"),
-    "S0": ("psum", [128, 1024], "float32"),
-    "S1": ("psum", [128, 1024], "float32"),
-    "S2": ("psum", [128, 1024], "float32"),
-    "S3": ("psum", [128, 1024], "float32"),
+    "KS": ("psum", [128, 1024], "float32"),
+    "E0": ("psum", [128, 512], "float32"),
+    "E1": ("psum", [128, 512], "float32"),
+    "E2": ("psum", [128, 512], "float32"),
+    "E3": ("psum", [128, 512], "float32"),
+    "E4": ("psum", [128, 32, 16], "float32"),
+    "PM": ("psum", [128, 6, 72], "float32"),
 }
 for _names, _shape, _dt in [
         ("Y", [4, 64], "int32"), ("Yb Yw Yj", [4, 64], "bfloat16"), ("W", [2048], "bfloat16"),
-        ("S32", [512], "int32"), ("S16 PL IL", [512], "uint16"), ("ILi", [4, 2, 64], "int32"),
-        ("P TT R", [8192], "bfloat16"), ("G", [4096], "bfloat16"),
-        ("KI", [4], "int32"), ("CI", [8], "int32"), ("CF", [16], "float32"), ("J32", [36], "float32"),
-        ("JP JH VAL HM B1 B2 E EI E1 E2", [32], "float32"), ("NE", [4], "float32"),
-        ("BI BSE C ONE IDN TRI SWF OD GD DT0 DT1", [128], "bfloat16"),
-        ("SELI", [32, 128], "bfloat16"), ("SEL", [NA, 128], "bfloat16"), ("SW", [4, 128], "bfloat16"),
-        ("Z", [224], "bfloat16"), ("R1 R2", [32], "bfloat16"), ("MSK", [512], "float32"), ("MA MW", [2], "float32"),
-        ("SC", [2, 512], "float32"), ("KY KO KB", [2, 32], "int32"), ("KR DL GO", [2, 32], "float32"),
-        ("CP", [4, 32], "bfloat16"), ("O", [256], "float32"), ("ACC", [8], "float32"), ("CL", [4, 4], "float32")]:
+        ("S32 NL", [4, 128], "int32"), ("S16 PL", [512], "uint16"), ("IL", [2, 256], "uint16"),
+        ("OFF", [32], "uint16"), ("P R", [8192], "bfloat16"), ("TT WT", [WIN], "bfloat16"), ("G P2", [4096], "bfloat16"),
+        ("MX", [4, 128], "float32"), ("KI", [4], "int32"), ("CI", [8], "int32"), ("CF", [24], "float32"), ("J32", [36], "float32"),
+        ("JP JH B1 B2 EI EA EB", [32], "float32"), ("NE MZ", [4], "float32"),
+        ("BI C C2 ONE IDN NID TRI SH BD NBD D512 PERM IOTA OS BT DT DNZ RS S0", [128], "bfloat16"),
+        ("SELI", [32, 128], "bfloat16"), ("SW SELD", [4, 128], "bfloat16"), ("U", [8, 128], "bfloat16"),
+        ("Z R1 R2 MK8", [32], "bfloat16"), ("CC", [16, 2], "bfloat16"), ("SP", [8, 16], "bfloat16"), ("SQ", [2, 16], "bfloat16"),
+        ("DS DG", [512], "bfloat16"), ("KC", [256], "bfloat16"), ("ZR", [288], "bfloat16"),
+        ("MSK", [256], "float32"), ("MW", [2], "float32"), ("NG", [1], "float32"),
+        ("SC", [1024], "float32"), ("KR ZZ", [64], "float32"), ("NS", [72], "float32"),
+        ("FF LL TL BB OWN BST GO DL GD", [64], "bfloat16"), ("SB", [88], "bfloat16"), ("SI TM", [288], "float32"),
+        ("ST", [128], "float32"), ("X32", [4, 132], "float32"), ("MD", [4, 8, 9], "float32"), ("OM", [6, 8, 9], "bfloat16"),
+        ("M1", [2, 6, 8, 9], "bfloat16"), ("M2", [2, 4, 8, 9], "bfloat16"),
+        ("NPO LO", [4, 2, 16], "float32"), ("ACC", [12], "float32"), ("CL", [4, 4], "float32")]:
     for _n in _names.split():
         SCRATCH[_n] = ("sbuf", [128] + _shape, _dt)
-SEMAPHORES = (["ev", "ea", "et", "eg", "dy", "dyo", "dp", "di", "dio", "do", "dn", "dc", "ca", "sent"]
+SEMAPHORES = (["ev", "ea", "et", "eg", "dy", "dyo", "dp", "di", "dio", "dt", "w1", "w2", "w3", "dn", "dc", "ca", "sent"]
               + ["%s%d" % (n, q) for n in ("ya", "pa", "ia", "oa", "dw") for q in range(4)])
 
 
@@ -59,7 +65,7 @@ def rank_program(g, core, T, topo):
                 clock[q][k] = ck[k]
 
     def deps(q, reads, writes):
-        toks = [wr[k] for k in list(reads) + list(writes) if k in wr]
+        toks = [wr[k] for k in list(reads) + list(writes) if k in wr and not (k[:1] == ("B",) and wr[k][3] == q)]
         for k in writes:
             toks += rd.get(k, [])
         toks.sort(key=lambda t: -(t[1] if t[1] is not None else cnt[t[0]]))
@@ -101,11 +107,17 @@ def rank_program(g, core, T, topo):
     def tt(out, a, b, o, reads, writes):
         op("v", lambda: V.tensor_tensor(out, a, b, o), reads, writes)
 
+    def scan(out, a, b, o0, o1, reads, writes):
+        op("v", lambda: V.tensor_tensor_scan(out, a, b, 0.0, o0, o1), reads, writes)
+
+    def act(out, in_, f, reads, writes, **kw):
+        op("a", lambda: S.activation(out, in_, f, **kw), reads, writes)
+
     def cp(q, out, in_, reads, writes):
         if q == "v":
             op("v", lambda: V.tensor_copy(out, in_), reads, writes)
         else:
-            op("a", lambda: S.activation(out, in_, F.Copy), reads, writes)
+            act(out, in_, F.Copy, reads, writes)
 
     def mm(out, l, r, st, sp, reads, writes):
         op("t", lambda: PE.matmul(out, l, r, st, sp), reads, writes)
@@ -115,12 +127,12 @@ def rank_program(g, core, T, topo):
 
     def io(out, pat, base, cm, writes, flag=True):
         if flag:
-            op("g", lambda: g.iota(out, pat, base, cm, allow_small_or_imprecise_dtypes=True), [], writes + ["POOL"])
+            op("g", lambda: g.iota(out, pat, base, cm, allow_small_or_imprecise_dtypes=True), ["POOL"], writes)
         else:
-            op("g", lambda: g.iota(out, pat, base, cm), [], writes + ["POOL"])
+            op("g", lambda: g.iota(out, pat, base, cm), ["POOL"], writes)
 
     def af(out, in_, pat, cmp, fill, base, cm, reads, writes):
-        op("g", lambda: g.affine_select(out, in_, pat, cmp, fill, base, cm), reads, writes + ["POOL"])
+        op("g", lambda: g.affine_select(out, in_, pat, cmp, fill, base, cm), reads + ["POOL"], writes)
 
     def hops(a, b):
         ca, cb = topo.chip(cores[a]), topo.chip(cores[b])
@@ -156,7 +168,7 @@ def rank_program(g, core, T, topo):
     for b in others:
         lands(("Y", b), "ya%d" % b, len(topo.engines(cores[b], core)))
         lands(("PL", b), "pa%d" % b, len(share(b, 0)[me]))
-        lands(("ILi", b), "ia%d" % b, len(share(b, 1)[me]))
+        lands(("NL", b), "ia%d" % b, len(share(b, 1)[me]))
         lands(("LO", b), "oa%d" % b, len(share(b, 1)[me]))
         lands("CLfar", "ca", sum(len(x) for x in share(b, 0).values()))
 
@@ -167,31 +179,33 @@ def rank_program(g, core, T, topo):
     dma("a", T.Y[64:128, me, :], T.w[2 * me:2 * me + 2, :], "dyo", [], ["Yown"])
     for r in range(4):
         for i in range(4):
-            dma("s" if i < 2 else "a", T.S32[32 * i:32 * i + 32, 128 * r:128 * r + 128],
-                T.pin[32 * r:32 * r + 32, 128 * i:128 * i + 128], "dp", [], [("S32", r, i)])
+            dma("sa"[i // 2], T.S32[32 * i:32 * i + 32, r, :], T.pin[32 * r:32 * r + 32, 128 * i:128 * i + 128], "dp", [], [("S32", r, i)])
     S32K = [("S32", r, i) for r in range(4) for i in range(4)]
 
     io(T.KI[:, 0:1], [[0, 1]], 0, 1, ["KI"], False)
     io(T.J32[:], [[1, 36]], 0, 0, ["J32"])
     io(T.JH[:], [[1, 2], [0, 16]], 0, 0, ["JH"])
     io(T.JP[:], [[0, 2], [1, 16]], 0, 0, ["JP"])
+    io(T.ONE[:], [[0, 128]], 1, 0, ["ONE"])
+    io(T.IOTA[:], [[1, 128]], 0, 0, ["IOTA"])
+    io(T.CF[:, 16:17], [[0, 1]], 1, 1, ["c16"])
     deps("g", DYK, [])
     for b in others:
         rid, pid, _e = topo.addr(cores[b])
         g.remote_dma(T.Y[:, me, :], T.DY[b], T.sem["ya%d" % me], T.sem.sent, pid, rid, topo.mask(core, cores[b]))
         cnt["sent"] += len(topo.engines(core, cores[b]))
 
-    for j, (sh_, an) in enumerate([(0, 31), (5, 3), (0, 15), (1, 1), (0, 1), (2, NA - 1), (4, 1)]):
+    for j, (sh_, an) in enumerate([(0, 31), (5, 3), (0, 15)]):
         ts(T.CI[:, j:j + 1], T.KI[:, 0:1], sh_, an, A.logical_shift_right, A.bitwise_and, ["KI"], [("CI", j)])
     ms(T.Yb[64:128], 1.0, ["Yb1"])
-    cp("v", T.CF[:, 0:7], T.CI[:, 0:7], [("CI", j) for j in range(7)], ["CF"])
+    cp("v", T.CF[:, 0:3], T.CI[:, 0:3], [("CI", j) for j in range(3)], ["CF"])
 
     def col(j):
         return T.CF[:, j:j + 1]
 
-    def scaled(j, out, in_, c, reads, writes):
-        if j % 4 == 3:
-            op("a", lambda: S.activation(out, in_, F.Identity, scale=c), reads, writes)
+    def scaled(e, out, in_, c, reads, writes):
+        if e == "a":
+            act(out, in_, F.Identity, reads, writes, scale=c)
         else:
             ts(out, in_, c, None, A.mult, None, reads, writes)
     ts(col(14), col(1), 2.0, None, A.is_equal, None, ["CF"], ["c14"])
@@ -199,11 +213,12 @@ def rank_program(g, core, T, topo):
     ts(T.EI[:], T.J32[:, 0:32], col(0), None, A.is_equal, None, ["J32", "CF"], ["EI"])
     ts(T.B1[:], T.JH[:], col(1), 2.0, A.is_equal, A.mult, ["JH", "CF"], ["B1"])
     ts(T.B2[:], T.JP[:], col(15), col(14), A.mult, A.add, ["JP", "c14", "c15"], ["B2"])
+    ts(col(11), col(2), 0.0, None, A.is_equal, None, ["CF"], ["c11"])
     for i in range(4):
         tt(T.BI[:, 32 * i:32 * i + 32], T.B1[:], T.B2[:], A.add, ["B1", "B2"], [("BI", i)])
     for a in range(32):
-        scaled(a, T.SELI[:, a, :], T.BI[:], T.EI[:, a:a + 1], [("BI", i) for i in range(4)] + ["EI"], [("SELI", a)])
-    SELK = [("SEL", a) for a in range(NA)]
+        scaled("a" if a % 5 in (1, 3) else "v", T.SELI[:, a, :], T.BI[:], T.EI[:, a:a + 1],
+               [("BI", i) for i in range(4)] + ["EI"], [("SELI", a)])
     CK = [("C", i) for i in range(4)]
 
     def pins():
@@ -211,273 +226,381 @@ def rank_program(g, core, T, topo):
         fused(0, "pa", lambda b: T.S16[:, 128 * b:128 * b + 128], T.PL[:, 128 * me:128 * me + 128], ["S16"])
 
     def more():
-        cp("v", T.PL[:, 128 * me:128 * me + 128], T.S16[:, 128 * me:128 * me + 128], ["S16"], [("PL", me)])
-        ms(T.Z[:], 0.0, ["Z"])
-        ts(col(11), col(2), 0.0, None, A.is_equal, None, ["CF"], ["c11"])
-        ts(col(8), col(4), -2.0, None, A.mult, None, ["CF"], ["c8"])
-        ts(col(9), col(4), -1.0, 2.0, A.mult, A.add, ["CF"], ["c9"])
         ts(col(12), col(11), 16.0, col(0), A.mult, A.add, ["c11", "CF"], ["c12"])
         ts(col(13), col(11), -16.0, 8.0, A.mult, A.add, ["c11"], ["c13"])
-        ts(T.E1[:], T.EI[:], -8.0, None, A.mult, None, ["EI"], ["E1"])
+        scaled("a", T.EA[:], T.EI[:], -8.0, ["EI"], ["EA"])
         ts(T.NE[:], T.J32[:, 0:4], col(1), None, A.not_equal, None, ["J32", "CF"], ["NE"])
-        ts(T.E2[:], T.J32[:, 1:33], col(12), col(13), A.is_equal, A.mult, ["J32", "c12", "c13"], ["E2"])
-        ts(T.HM[:], T.JH[:], col(3), None, A.is_equal, None, ["JH", "CF"], ["HM"])
-        tt(T.Z[:, 96:128], T.E1[:], T.E2[:], A.add, ["E1", "E2"], ["Z"])
-        ts(T.VAL[:], T.JP[:], col(8), col(9), A.mult, A.add, ["JP", "c8", "c9"], ["VAL"])
-        for i in range(4):
-            scaled(3, T.C[:, 32 * i:32 * i + 32], T.Z[:, 96:128], T.NE[:, i:i + 1], ["Z", "NE"], [("C", i)])
-        ts(T.E[:, 0:NA], T.J32[:, 0:NA], col(5), None, A.is_equal, None, ["J32", "CF"], ["E"])
-        for i in range(4):
-            tt(T.BSE[:, 32 * i:32 * i + 32], T.VAL[:], T.HM[:], A.mult, ["VAL", "HM"], [("BSE", i)])
-        ts(T.R1[:], T.EI[:], 1024.0, None, A.mult, None, ["EI"], ["R1"])
-        ts(T.MA[:], T.J32[:, 0:2], col(6), -1.0, A.is_equal, A.mult, ["J32", "CF"], ["MA"])
+        ts(T.EB[:], T.J32[:, 1:33], col(12), col(13), A.is_equal, A.mult, ["J32", "c12", "c13"], ["EB"])
+        cp("v", T.PL[:, 128 * me:128 * me + 128], T.S16[:, 128 * me:128 * me + 128], ["S16"], [("PL", me)])
+        tt(T.Z[:], T.EA[:], T.EB[:], A.add, ["EA", "EB"], ["Z"])
+        ts(T.MZ[:], T.J32[:, 0:4], col(1), None, A.is_equal, None, ["J32", "CF"], ["MZ"])
         ts(T.MW[:], T.J32[:, 2:4], col(1), 15.0, A.is_equal, A.mult, ["J32", "CF"], ["MW"])
-        for a in range(NA):
-            scaled(3, T.SEL[:, a, :], T.BSE[:], T.E[:, a:a + 1], [("BSE", i) for i in range(4)] + ["E"], [("SEL", a)])
-        ms(T.CL[:, me, :], 0.0, ["CLown"])
+        scaled("a", T.R1[:], T.EI[:], 2048.0, ["EI"], ["R1"])
+        for i in range(4):
+            scaled("a", T.C[:, 32 * i:32 * i + 32], T.Z[:], T.NE[:, i:i + 1], ["Z", "NE"], [("C", i)])
 
-    SL = [T.S0, T.S1, T.S2, T.S3]
+    BANK = [T.KS[:, 0:512], T.KS[:, 512:1024], T.E0[:], T.E1[:], T.E2[:], T.E3[:], T.E4[:]]
+    TURN = [0, 1, 2, 3, 4, 6]
 
-    def banks(k):
-        return [("B", 2 * k), ("B", 2 * k + 1)]
+    def bk(k):
+        return [("B", k)]
 
-    def sign(q, out, k, y, writes):
-        src, bk = (SL[k][:], banks(k)) if y is None else (SL[k][:, 512 * y:512 * y + 512], [("B", 2 * k + y)])
+    def part(k, a, b):
+        return T.E4[:, a // 16:b // 16, :] if k == 6 else T.PM[:, a // 64:b // 64, 0:64] if k == 7 else BANK[k][:, a:b]
+
+    def sign(q, out, k, writes):
         if q == "v":
-            ts(out, src, -1.0, 1.0, A.max, A.min, [], writes + bk)
+            ts(out, BANK[k], -1.0, 1.0, A.max, A.min, [], writes + bk(k))
         else:
-            op("a", lambda: S.activation(out, src, F.Sign), [], writes + bk)
+            act(out, BANK[k], F.Sign, [], writes + bk(k))
 
-    PK = [("P", q, x) for q in range(4) for x in range(4)]
-    RK = [("R", q, x) for q in range(4) for x in range(2)]
+    PK = [("P", c) for c in range(16)]
+    RK = [("R", c) for c in range(16)]
+    TK = [("TT", c) for c in range(16)]
+
+    def narrow(j):
+        q = order[j]
+        cp("v", T.Yb[0:64, q, :], T.Y[0:64, q, :], [("Y", q)], [("Yb", q)])
 
     def take(j):
         q = order[j]
-        cp("v", T.Yb[0:64, q, :], T.Y[0:64, q, :], [("Y", q)], [("Yb", q)])
+        if j < 2:
+            narrow(j)
         for y in range(4):
-            k = 2 * (j % 2) + y // 2
+            k = (4 * j + y) % 7
             for al in range(8 * y, 8 * y + 8):
-                c0 = 64 * (al % 16)
-                mm(SL[k][:, c0:c0 + 64], T.SELI[0:96, al, :], T.Yb[0:96, q, :], True, True,
-                   [("SELI", al), ("Yb", q), "Yb1"], [("B", 2 * k + y % 2)])
-        cp("v", T.Yw[64:128, q, :], T.Y[64:128, q, :], [("Y", q), "Yown"], [("Yw", q)])
+                c0 = 64 * (al % 8)
+                mm(part(k, c0, c0 + 64), T.SELI[0:96, al, :], T.Yb[0:96, q, :], True, True,
+                   [("SELI", al), ("Yb", q), "Yb1"], bk(k))
+            if y == 0:
+                cp("v", T.Yw[64:128, q, :], T.Y[64:128, q, :], [("Y", q), "Yown"], [("Yw", q)])
+            if y == 3 and j in (1, 2):
+                narrow(j + 1)
+            if j > 0:
+                put(j, y)
         for h in range(2):
             dma("s", T.W[2 * q + h:2 * q + h + 1, :], T.Yw[64 + 32 * h:96 + 32 * h, q, :], "dw%d" % q, [("Yw", q)], [("W", q, h)])
 
-    def put(j):
+    def put(j, y):
         q = order[j]
-        for y in range(4):
-            sign("av"[y % 2], T.P[:, 2048 * q + 512 * y:2048 * q + 512 * y + 512], 2 * (j % 2) + y // 2, y % 2, [("P", q, y)])
-    take(0); pins(); put(0); more(); take(1); take(2); put(1); take(3); put(2); put(3)
-    WK = [("W", q, h) for q in range(4) for h in range(2)]
-    for i in range(4):
-        for pi in range(2):
-            dma("s", T.DI[:, 32 * i:32 * i + 32, 64 * pi:64 * pi + 64], T.inc[pi::2, 128 * i:128 * i + 128],
-                "di", [], [("DI", i, pi)])
-    DIK = [("DI", i, pi) for i in range(4) for pi in range(2)]
-    dma("s", T.ILi[:, me], T.DI[me], "dio", DIK, [("ILi", me)])
+        sign("av"[y % 2], T.P[:, 2048 * q + 512 * y:2048 * q + 512 * y + 512], (4 * j + y) % 7, [("P", 4 * q + y)])
 
-    io(T.ONE[:], [[0, 128]], 1, 0, ["ONE"])
+    take(0); pins()
+    for y in range(4):
+        put(0, y)
+    more()
+    take(1)
+    for i in range(4):
+        dma("s", T.DI[:, 32 * i:32 * i + 32, :], T.inc[:, 128 * i:128 * i + 128], "di", [], [("DI", i)])
+    take(2); take(3)
+    for i in range(4):
+        dma("s", T.NL[32 * i:32 * i + 32, me, :], T.inc[32 * me:32 * me + 32, 128 * i:128 * i + 128], "dio", [], [("NL", me, i)])
+    NLK = [("NL", q) for q in others] + [("NL", me, i) for i in range(4)]
+    WK = [("W", q, h) for q in range(4) for h in range(2)]
+
+    def diag(out, base, fill, key, src=None):
+        if src is None:
+            af(out, T.ONE[:], [[-1, 128]], A.is_equal, 0.0, base, 1, ["ONE"], [key])
+        else:
+            af(out, T[src][:], [[-1, 128]], A.not_equal, fill, base, 1, [src], [key])
     for q in order:
         af(T.SW[0:8, q, :], T.ONE[0:8, :], [[0, 4], [-1, 2], [0, 16]], A.is_equal, 0.0, -2 * q, 1, ["ONE"], [("SW", q)])
+    io(T.ST[:], [[0, 128]], 1, 0, [("ST", z) for z in range(4)])
+    io(T.MD[:, 0:2], [[0, 144]], 0, 0, [("MD", 0), ("MD", 1)])
+    io(T.WT[:, 0:SEED], [[0, SEED]], 1, 0, [("WT", 0)])
+    for j in range(4):
+        af(T.MX[:, j, :], T.ST[:], [[-16, 8], [1000, 2], [-2, 8]], A.is_equal, 0.0, -(j // 2) - 1000 * (j % 2), 1,
+           [("ST", 0)], [("MX", j)])
+    fused(1, "ia", lambda b: T.DI[b], T.NL[:, me], [("DI", i) for i in range(4)])
+    for x in range(2):
+        for pi in range(2):
+            v_ = T.MD[:, pi, :, 1 - x:9 - x]
+            af(v_, v_, [[-16, 8], [-2, 8]], A.not_equal, 1.0 - 2 * x, -pi, 1, [("MD", pi)], [("MD", pi)])
+    io(T.X32[:, :, 0], [[0, 4]], 0, 0, ["X0"])
+    io(T.ZR[0:1, :], [[0, 288]], 0, 0, ["ZR"])
     hp = [[-16, 2], [0, 16]]
     r2 = [T.R2[32 * j:32 * j + 32, :] for j in range(4)]
-    io(r2[0], [[0, 32]], 1, 0, [("R2", 0)])
-    io(r2[1], [[0, 2], [32, 16]], 512, 0, [("R2", 1)])
-    io(r2[2], [[0, 2], [-16, 16]], -256, 0, [("R2", 2)])
-    io(r2[3], [[0, 2], [16, 16]], 256, 0, [("R2", 3)])
-    af(r2[0], r2[0], hp, A.not_equal, 15.0, 0, 1, [("R2", 0)], [("R2", 0)])
-    af(r2[1], r2[1], hp, A.is_equal, 0.0, 0, 1, [("R2", 1)], [("R2", 1)])
-    af(r2[2], r2[2], [[-1, 32]], A.is_equal, 0.0, 0, 1, [("R2", 2)], [("R2", 2)])
-    af(r2[3], r2[3], [[-1, 32]], A.is_equal, 0.0, -1, 1, [("R2", 3)], [("R2", 3)])
-    af(r2[0], r2[0], hp, A.is_ge, 0.0, 0, 1, [("R2", 0)], [("R2", 0)])
+    io(T.R2[0:64, :], [[0, 32]], 0, 0, [("R2", 0), ("R2", 1)])
+    af(r2[0], r2[0], [[16, 2], [0, 16]], A.is_ge, 0.5, 0, -1, [], [("R2", 0)])
+    io(T.KC[0:1, :], [[0, 16], [32, 16]], 1056, 0, ["KC"])
+    af(r2[0], r2[0], [[16, 2], [0, 16]], A.is_ge, 0.0, 15, -1, [], [("R2", 0)])
+    io(r2[2], [[0, 2], [-16, 16]], -528, 0, [("R2", 2), "POOL"])
+    io(r2[3], [[0, 2], [16, 16]], 528, 0, [("R2", 3), "POOL"])
+    af(r2[1], r2[1], hp, A.not_equal, 7.5, 0, 1, [], [("R2", 1), "POOL"])
+    af(r2[2], r2[2], [[-1, 32]], A.is_equal, 0.0, 0, 1, [], [("R2", 2), "POOL"])
+    af(r2[3], r2[3], [[-1, 32]], A.is_equal, 0.0, -1, 1, [], [("R2", 3), "POOL"])
     last = T.R2[96:128, 15::16]
-    io(last, [[0, 2]], -496, 0, [("R2", 3)])
-    af(r2[0], r2[0], [[16, 2], [0, 16]], A.is_ge, 0.0, 15, -1, [("R2", 0)], [("R2", 0)])
-    af(last, last, [[-16, 2]], A.is_equal, 0.0, 0, 1, [("R2", 3)], [("R2", 3)])
+    io(last, [[0, 2]], -768, 0, [("R2", 3), "POOL"])
+    af(last, last, [[-16, 2]], A.is_equal, 0.0, 0, 1, [], [("R2", 3), "POOL"])
     R2K = [("R2", j) for j in range(4)]
-    io(T.MSK[:], [[0, 512]], 131072, 0, ["MSK"])
-    fused(1, "ia", lambda b: T.DI[b], T.ILi[:, me], DIK)
-    af(T.MSK[:], T.MSK[:], [[0, 32], [1, 16]], A.is_equal, 0.0, 0, 0, ["MSK"], ["MSK"])
-    io(T.CP[:], [[0, 128]], 0, 0, [("CP", 0), ("CP", 1)])
+    io(T.MSK[:], [[0, 256]], 0, 0, ["MSK"])
+    diag(T.IDN[:], 0, None, "IDN")
+    io(T.MSK[:, 0::16], [[0, 16]], 262144, 0, ["MSK"])
+    io(T.OM[0:2], [[0, 432]], 0, 0, ["OM"])
+    io(T.OS[0:2, :], [[1, 128]], 0, 0, ["OS"])
+    io(T.OM[0:2, 2:6, :, 0], [[0, 8], [128, 4]], 8192, 0, ["OM"])
+    af(T.OS[0:2, :], T.OS[0:2, :], [[0, 128]], A.is_equal, 1.0, 0, 1, ["OS"], ["OS"])
+    af(T.OM[0:2, 2:6, :, 0], T.OM[0:2, 2:6, :, 0], [[0, 32]], A.not_equal, 1.0, 0, 1, ["OM"], ["OM"])
+    af(T.MK8[:], T.ONE[:, 0:32], [[0, 4], [1, 8]], A.not_equal, 0.0, 0, 0, ["ONE"], ["MK8"])
+    io(T.OM[0:2, 0, :, 0], [[0, 8]], 1, 0, ["OM"])
     af(T.TRI[:], T.ONE[:], [[1, 128]], A.is_gt, 0.0, 0, -1, ["ONE"], ["TRI"])
-    af(T.TRI[:], T.TRI[:], [[1, 128]], A.not_equal, -512.0, 0, -1, ["TRI"], ["TRI"])
-    io(T.OD[:], [[0, 128]], 1, 0, [("OD", 0), ("OD", 1)])
-    io(T.GD[:], [[0, 128]], 0, 0, [("GD", 0), ("GD", 1)])
-    af(T.IDN[:], T.ONE[:], [[-1, 128]], A.is_equal, 0.0, 0, 1, ["ONE"], ["IDN"])
-    af(T.SWF[0:8, :], T.ONE[0:8, :], [[-1, 8], [0, 16]], A.is_equal, 0.0, 0, 1, ["ONE"], ["SWF"])
+    diag(T.SH[:], 1, None, "SH")
+    diag(T.BD[:], 1, -1.0, "BD", "IDN")
+    diag(T.NBD[:], 0, -1.0, "NBD", "SH")
+    diag(T.D512[:], 0, -512.0, "D512", "IDN")
+    io(T.S0[0:9, :], [[0, 8], [-32, 16]], 1008, 0, ["S0"])
+    af(T.PERM[:], T.ONE[:], [[-1, 32], [-32, 4]], A.is_equal, 0.0, 0, 1, ["ONE"], ["PERM"])
+    af(T.S0[0:9, :], T.S0[0:9, :], [[0, 128]], A.is_equal, 0.0, 0, 1, ["S0"], ["S0"])
+    io(T.SB[:, 8:9], [[0, 1]], 1, 0, ["SB0"])
+    for q in range(4):
+        af(T.SELD[0:9, q, :], T.S0[0:9, :], [[0, 4], [-4, 2], [0, 16]], A.not_equal, 1.0, -1 - q, 1, ["S0"], [("SELD", q)])
+    io(T.DT[64:96, :], [[0, 128]], 1, 0, ["DT1", "POOL"])
+    af(T.DNZ[:], T.IDN[:], [[0, 8], [1, 16]], A.not_equal, 0.0, 0, 0, ["IDN"], ["DNZ"])
+    af(T.RS[0:4, :], T.ONE[0:4, :], [[-1, 128]], A.is_equal, 0.0, 0, 16, ["ONE"], ["RS"])
+    af(T.SP[0:4], T.ONE[0:4, :], [[0, 4], [-1, 2], [0, 16]], A.is_equal, 0.0, 0, 1, ["ONE"], ["SP"])
+    af(T.SQ[0:4], T.ONE[0:4, 0:32], [[-1, 2], [0, 16]], A.is_equal, 0.0, 0, 1, ["ONE"], ["SQ"])
+    af(T.SP[0:4, :, 0::15], T.SP[0:4, :, 0::15], [[0, 4], [-1, 2], [0, 2]], A.not_equal, -24.0, -2, 1, ["SP"], ["SP"])
+    af(T.SQ[0:4, :, 0::15], T.SQ[0:4, :, 0::15], [[-1, 2], [0, 2]], A.not_equal, -32.0, -2, 1, ["SQ"], ["SQ"])
+    io(T.NG[:], [[0, 1]], -1, 0, ["NG"])
+    io(T.CL[:, me, :], [[0, 4]], 0, 0, ["CLown"])
 
-    def gather_pin(e, c0, m, key):
-        cp(e, T.TT[:, c0:c0 + m], T.P[:, 0:8192].indirect(T.PL[:, c0 // 16:(c0 + m) // 16]), PK + [("PL", c0 // 2048)], key)
+    for j in range(1, 4):
+        dma("s", T.WT[:, SEED * j:SEED * j + SEED], T.WT[:, 0:SEED], "w1", [("WT", 0)], [("WT", j)])
+    for j in range(1, 4):
+        dma("s", T.WT[:, 4 * SEED * j:4 * SEED * (j + 1)], T.WT[:, 0:4 * SEED], "w2", [("WT", x) for x in range(4)], [("WT", 3 + j)])
+    WTK = [("WT", x) for x in range(7)]
+    for h in range(2):
+        dma("s", T.WT[16 * h:16 * h + 1, 0:8192], T.W[h:8:2, :], "w3", WK, WTK if h == 0 else ["WTb"])
 
-    def lists(pi):
-        cp("v", T.IL[:, 256 * pi:256 * pi + 256], T.ILi[:, :, pi, :], [("ILi", q) for q in range(4)], [("IL", pi)])
+    def lists_mm(pi, k, x):
+        mm(part(k, 0, 256), T.MX[:, 2 * pi + x, :], T.X32[:, :, 1 + x:129:2], x == 0, x == 1, [("MX", 2 * pi + x), "X32"], bk(k))
 
+    def lists(pi, k):
+        cp("v", T.IL[:, pi], part(k, 0, 256), [], [("IL", pi)] + bk(k))
+
+    def numbers():
+        cp("v", T.X32[:, :, 1:129], T.NL[:], NLK, ["X32"])
+        act(T.MD[:, 2:4], T.MD[:, 0:2], F.Identity, [("MD", 0), ("MD", 1)], ["MDn"], scale=-1.0)
+
+    def steps_mm(pi, qs, close=True):
+        for q in qs:
+            if q == 0:
+                mm(T.E3[:, 0:288], T.ONE[0:1, :], T.ZR[0:1, :], True, False, ["ONE", "ZR"], bk(5))
+            o = T.E3[:, 72 * q:72 * q + 72]
+            mm(o, T.X32[:, q, 1:129], T.MD[:, pi], False, False, ["X32", ("MD", pi)], bk(5))
+            mm(o, T.X32[:, q, 0:128], T.MD[:, 2 + pi], False, close and q == 3, ["X0", "MDn"], bk(5))
+
+    def steps_high(pi):
+        act(T.TM[:], T.E3[:, 0:288], F.Identity, [], ["TM"] + bk(5), bias=R128)
+        steps_mm(pi, range(4), False)
+        for q in range(4):
+            act(T.M1[:, pi, 2:6, q::4, :], T.TM[:, 72 * q:72 * q + 72], F.Identity, ["TM"], [("M1", pi, q)], bias=-R128)
+        for q in range(4):
+            mm(T.E3[:, 72 * q:72 * q + 72], T.NID[:], T.M1[:, pi, 2:6, q::4, :], False, q == 3, ["NID", ("M1", pi, q)], bk(5))
+
+    def steps_low(pi):
+        for q in range(4):
+            cp("a", T.M2[:, pi, :, q::4, :], T.E3[:, 72 * q:72 * q + 72], [], [("M2", pi, q)] + bk(5))
+
+    def relu(e, c, k):
+        o = T.R[:, 512 * c:512 * c + 512]
+        if e == "v":
+            ts(o, BANK[k], 0.0, None, A.max, None, [], [("R", c)] + bk(k))
+        else:
+            act(o, BANK[k], F.Relu, [], [("R", c)] + bk(k))
+
+    def edges_first():
+        cs = [4 * q + y for q in order for y in range(4)]
+
+        def fetch(j):
+            c, k = cs[j], TURN[j % 6]
+            cp("va"[j % 2], T.TT[:, 512 * c:512 * c + 512], T.P[:, 0:8192].indirect(T.PL[:, 32 * c:32 * c + 32]),
+               PK + [("PL", c // 4)], [("TT", c)])
+            mm(BANK[k], T.SW[0:8, c // 4, :], T.W[0:8, 512 * (c % 4):512 * (c % 4) + 512], True, False, WK + [("SW", c // 4)], bk(k))
+            mm(BANK[k], T.C[:], T.TT[:, 512 * c:512 * c + 512], False, True, CK + [("TT", c)], bk(k))
+        for j in range(20):
+            if j < 16:
+                fetch(j)
+            if j == 12:
+                numbers(); lists_mm(0, 7, 0)
+            if j == 13:
+                lists_mm(0, 7, 1)
+            if j == 16:
+                lists(0, 7); steps_mm(0, range(4))
+            if j >= 4:
+                relu("a" if j == 16 else "va"[j % 2], cs[j - 4], TURN[(j - 4) % 6])
+        for h in range(2):
+            dma("s", T.TT[16 * h:16 * h + 1, 0:8192], T.W[h:8:2, :], "dt", WK, TK if h == 0 else ["TTb"])
+
+    def edges_again():
+        for c in range(16):
+            mm(BANK[TURN[c % 6]], T.C2[:], T.TT[:, 512 * c:512 * c + 512], True, True, ["C2"] + TK, bk(TURN[c % 6]))
+            relu("va"[c % 2], c, TURN[c % 6])
+
+    def spread(y):
+        k = (3, 6)[y % 2]
+        for a in range(4 * y, 4 * y + 4):
+            c0 = 128 * (a % 4)
+            mm(part(k, c0, c0 + 128), T.SELI[0:96, a, :], T.DT[0:96, :], True, True, [("SELI", a), "DT", "DT1"], bk(k))
+        sign("a", T.P2[:, 512 * y:512 * y + 512], k, [("P2", y)])
+
+    CUT = [32, 32, 24, 24]
     for t in range(3):
         pi = t % 2
-        DT = T.DT1 if pi else T.DT0
+        if t == 0:
+            edges_first()
+        else:
+            edges_again()
 
-        def g1(j):
-            for x in range(2):
-                q = order[j]
-                gather_pin("va"[x], 2048 * q + 1024 * x, 1024, [("TT", q, 2 * x), ("TT", q, 2 * x + 1)])
+        def fetch(q):
+            for e, a, b in (("v", 0, CUT[q]), ("a", CUT[q], 64)):
+                cp(e, T.G[:, 1024 * q + 16 * a:1024 * q + 16 * b], T.R[:, 0:8192].indirect(T.IL[:, pi, 64 * q + a:64 * q + b]),
+                   RK + [("IL", pi)], [("G", q, e)])
 
-        def rec(j):
-            q = order[j]
-            for first in (True, False):
-                for x in range(2):
-                    k = 2 * x + j % 2
-                    for y in range(2):
-                        e0 = 1024 * x + 512 * y
-                        o = SL[k][:, 512 * y:512 * y + 512]
-                        if first:
-                            mm(o, T.SW[0:8, q, :], T.W[0:8, e0:e0 + 512], True, False, WK + [("SW", q)], [("B", 2 * k + y)])
-                        else:
-                            mm(o, T.C[:], T.TT[:, 2048 * q + e0:2048 * q + e0 + 512], False, True,
-                               CK + [("TT", q, 2 * x + y)], [("B", 2 * k + y)])
-
-        def relu(j):
-            q = order[j]
-            for x in range(2):
-                k = 2 * x + j % 2
-                o = T.R[:, 2048 * q + 1024 * x:2048 * q + 1024 * x + 1024]
-                if x == 0:
-                    ts(o, SL[k][:], 0.0, None, A.max, None, [], [("R", q, x)] + banks(k))
+        def keys(q, term):
+            if term == 0:
+                mm(BANK[q][:, 0:256], T.ONE[0:1, :], T.KC[0:1, :], True, False, ["ONE", "KC"], bk(q))
+            for c in range(8):
+                o = BANK[q][:, 32 * c:32 * c + 32]
+                if term == 1:
+                    mm(o, T.G[:, 1024 * q + c:1024 * q + 1024:8], T.R1[:], False, c == 7, [("G", q, "v"), ("G", q, "a"), "R1"], bk(q))
+                elif t < 2:
+                    mm(o, T.P[:, 2048 * q + 2 * c + pi:2048 * q + 2048:16], T.R2[:], False, False, PK + R2K, bk(q))
                 else:
-                    op("a", lambda: S.activation(o, SL[k][:], F.Relu), [], [("R", q, x)] + banks(k))
-        g1(0); rec(0); g1(1); rec(1); relu(0); g1(2); rec(2); relu(1); g1(3); rec(3); relu(2)
+                    a = 8 * q + c
+                    mm(o, T.P2[:, 128 * a:128 * a + 128], T.R2[:], False, False, [("P2", a // 4)] + R2K, bk(q))
+
+        def best(q):
+            scan(T.SC[:, 256 * q:256 * q + 256], T.MSK[:], BANK[q][:, 0:256], A.add, A.min, ["MSK"], [("SC", q)] + bk(q))
+
+        def aside(j):
+            if t == 0 and j < 2:
+                lists_mm(1, 6, j)
+            if t == 1:
+                steps_mm(1, [j] if j < 2 else [2, 3])
+
+        keys(0, 0); keys(1, 0)
+        fetch(0); keys(0, 1); keys(2, 0); aside(0)
+        fetch(1); keys(1, 1); keys(3, 0); aside(1); best(0)
+        fetch(2); keys(2, 1); aside(2); best(1)
+        mm(T.PM[:], T.OS[0:2, :], T.OM[0:2], True, False, ["OS", "OM"], bk(7))
+        fetch(3); keys(3, 1); best(2)
         if t == 0:
-            lists(0)
-        relu(3)
+            lists(1, 6)
+            act(T.NID[:], T.IDN[:], F.Identity, ["IDN"], ["NID"], scale=-1.0)
+        X = T.E4[:, 0:16, 0:9]
+        mm(X, T.ONE[0:1, :], T.ZR[0:1, 0:144], True, False, ["ONE", "ZR"], bk(6))
+        best(3)
+        if t < 2:
+            steps_high(pi)
 
-        def g2(e, u):
-            cp(e, T.G[:, 512 * u:512 * u + 512], T.R[:, 0:8192].indirect(T.IL[:, 256 * pi + 32 * u:256 * pi + 32 * u + 32]),
-               RK + [("IL", pi)], [("G", u)])
+        SCK = [("SC", q) for q in range(4)]
+        key = T.SC[:, 15::16]
+        ts(T.KR[:], key, R2048, -R2048, A.add, A.add, SCK, ["KR"])
+        tt(T.FF[:], T.KR[:], key, A.is_gt, SCK + ["KR"], ["FF"])
+        tt(T.ZZ[:], key, T.KR[:], A.subtract, SCK + ["KR"], ["ZZ"])
+        for h in range(2):
+            scan(T.LL[:, 32 * h:32 * h + 32], T.MK8[:], T.FF[:, h::2], A.mult, A.add, ["MK8", "FF"], [("LL", h)])
+        LK = [("LL", 0), ("LL", 1)]
+        nn = T.LL[:, 7::8]
+        mm(T.E0[:, 0:8], T.TRI[:], nn, True, True, ["TRI"] + LK, bk(2))
+        for c in range(8):
+            mm(T.E4[:, 0:8, 1 + c], T.SH[:], nn, False, False, ["SH"] + LK, bk(6))
+        ts(T.BB[:], T.ZZ[:], R32, -R32, A.add, A.add, ["ZZ"], ["BB"])
+        for h in range(2):
+            tt(T.TL[:, 32 * h:32 * h + 32], T.FF[:, h::2], T.LL[:, 32 * h:32 * h + 32], A.mult, ["FF", ("LL", h)], [("TL", h)])
+            mm(T.E4[:, 8 + 4 * h:12 + 4 * h, 1:9], T.BD[:], T.BB[:, h::2], False, False, ["BD", "BB"], bk(6))
+            mm(T.E4[:, 8 + 4 * h:12 + 4 * h, 0:8], T.NBD[:], T.BB[:, h::2], False, False, ["NBD", "BB"], bk(6))
+        mm(T.E4[:, 0:8, 1:9], T.BD[:], T.TL[:], False, True, ["BD", ("TL", 0), ("TL", 1)], bk(6))
+        if t < 2:
+            steps_low(pi)
+        cp("a", T.M1[:, pi, 0:2], X, [], [("M1d", pi)] + bk(6))
+        for u in range(8):
+            ts(T.U[:, u, :], T.IOTA[:], T.E0[:, u:u + 1], None, A.is_ge, None, ["IOTA"], [("U", u)] + bk(2))
+        for u in range(8):
+            mm(T.PM[:, 2:6, 9 * u:9 * u + 9], T.U[:, u, :], T.M2[:, pi, :, u, :], False, False, [("U", u), ("M2", pi, u % 4)], bk(7))
+            mm(T.PM[:, :, 9 * u:9 * u + 9], T.U[:, u, :], T.M1[:, pi, :, u, :], False, u == 7,
+               [("U", u), ("M1", pi, u % 4), ("M1d", pi)], bk(7))
+        mm(T.E2[:, 0:64], T.IDN[:], T.LL[:], True, False, ["IDN"] + LK, bk(4))
+        for h in range(2):
+            mm(T.E2[:, 32 * h:32 * h + 32], T.D512[:], T.FF[:, h::2], False, False, ["D512", "FF"], bk(4))
+        for c in range(8):
+            mm(T.E2[:, c:64:8], T.TRI[:], nn, False, c == 7, ["TRI"] + LK, bk(4))
+        for h in range(2):
+            tt(T.OWN[:, 32 * h:32 * h + 32], T.ZZ[:, h::2], T.BB[:, h::2], A.subtract, ["ZZ", "BB"], [("OWN", h)])
+            act(T.BST[:, 32 * h:32 * h + 32], T.BB[:, h::2], F.Identity, ["BB"], [("BST", h)], scale=1.0 / 32, bias=31.0)
+        OK = [("OWN", 0), ("OWN", 1)]
+        ts(T.NS[:], T.PM[:, 0, :], col(16), None, A.not_equal, None, ["c16"], ["NS"] + bk(7))
+        tt(T.DL[:], T.BST[:], T.OWN[:], A.subtract, [("BST", 0), ("BST", 1)] + OK, ["DL"])
+        scan(T.SB[:, 9:81], T.NS[:], T.PM[:, 1, :], A.mult, A.add, ["NS"], ["SB"] + bk(7))
+        mm(T.E0[0:9, 0:128], T.SB[:, 8:81:9], T.PERM[:], True, True, ["SB", "SB0", "PERM"], bk(2))
+        cp("a", T.BT[0:9, :], T.E0[0:9, 0:128], [], ["BT"] + bk(2))
+        for q in range(4):
+            mm(T.E4[:, :, 4 * q:4 * q + 4], T.SELD[0:9, q, :], T.BT[0:9, :], True, True, [("SELD", q), "BT"], bk(6))
+        sign("a", T.DS[:], 6, ["DS"])
+        for i in range(4):
+            scan(T.SI[:, 72 * i:72 * i + 72], T.NS[:], T.PM[:, 2 + i, :], A.mult, A.add, ["NS"], [("SI", i)] + bk(7))
+        ts(T.GO[:], T.E2[:, 0:64], -383.5, None, A.is_lt, None, [], ["GO"] + bk(4))
+        for z in range(4):
+            ts(T.ST[:, z::4], T.SI[:, 8::9], T.MZ[:, z:z + 1], None, A.mult, None, [("SI", i) for i in range(4)] + ["MZ"], [("ST", z)])
+        mm(T.E1[:, 0:32], T.ST[:], T.EI[:], True, True, [("ST", z) for z in range(4)] + ["EI"], bk(3))
+        tt(T.GD[:], T.GO[:], T.DL[:], A.mult, ["GO", "DL"], ["GD"])
+        cp("v", T.OFF[:], T.E1[:, 0:32], [], ["OFF"] + bk(3))
+        if t == 0:
+            mm(T.E2[0:64, 0:128], T.OWN[:], T.IDN[:], True, False, OK + ["IDN"], bk(4))
+            mm(T.E2[0:64, 0:128], T.GD[:], T.IDN[:], False, True, ["GD", "IDN"], bk(4))
+            cp("a", T.DT[0:64, :], T.E2[0:64, 0:128], [], ["DT"] + bk(4))
+            mm(BANK[1][:, 0:128], T.DNZ[:], T.C[:], True, False, ["DNZ"] + CK, bk(1))
+            mm(BANK[1][:, 0:128], T.RS[0:4, :], T.SP[0:4], False, True, ["RS", "SP"], bk(1))
+            cp("a", T.C2[:], BANK[1][:, 0:128], [], ["C2"] + bk(1))
+        else:
+            mm(T.E2[:, 0:64], T.IDN[:], T.OWN[:], True, False, OK + ["IDN"], bk(4))
+            mm(T.E2[:, 0:64], T.IDN[:], T.GD[:], False, True, ["GD", "IDN"], bk(4))
+            for h in range(2):
+                cp("a", T.NPO[:, :, h, pi::2], T.E2[:, 32 * h:32 * h + 32], [], [("NPO", pi, h)] + bk(4))
+        tt(T.DG[:], T.WT[:].indirect(T.OFF[:]), T.DS[:], A.mult, WTK + ["WTb", "OFF", "DS"], ["DG"])
+        cp("v", T.TT[:].indirect(T.OFF[:]), T.DG[:], ["DG", "OFF"], TK + ["TTb"])
+        if t < 2:
+            for y in range(4 * t, 4 * t + 4):
+                spread(y)
+        else:
+            mm(BANK[1][:, 0:32], T.DNZ[:], T.Z[:], True, False, ["DNZ", "Z"], bk(1))
+            mm(BANK[1][:, 0:32], T.RS[0:4, :], T.SQ[0:4], False, True, ["RS", "SQ"], bk(1))
+            for h in range(2):
+                cp("a", T.CC[:, :, h], BANK[1][:, 16 * h:16 * h + 16], [], [("CC", h)] + bk(1))
+            act(T.Yj[64:128], T.Yw[64:128], F.Identity, [("Yw", q) for q in range(4)], ["Yj", ("ACC", 8)], accum_out=T.ACC[64:128, 8:9])
 
-        def keys(u):
-            q, hf = u // 2, u // 4
-            for bb in range(2 * (u % 2), 2 * (u % 2) + 2):
-                for xb in range(2):
-                    blk = 4 * xb + bb
-                    c0 = 512 * hf + 32 * (8 * (q % 2) + blk)
-                    o = T.S0[:, c0:c0 + 32]
-                    p0 = 2048 * q + 256 * blk
-                    g0 = 1024 * q + 256 * bb
-                    mm(o, T.P[:, p0 + pi:p0 + 256:2], T.R2[:], True, False, PK + R2K, [("B", hf)])
-                    mm(o, T.G[:, g0 + xb:g0 + 256:2], T.R1[:], False, True, [("G", u), "R1"], [("B", hf)])
+    NK = [("NPO", pi, h) for pi in range(2) for h in range(2)]
+    fused(1, "oa", lambda b: T.NPO[:, b], T.LO[:, me], NK)
+    for b in order:
+        for h in range(2):
+            src, keys_ = (T.NPO[:, me, h, :], NK) if b == me else (T.LO[:, b, h, :], [("LO", b)])
+            dma("s", T.newpart[2 * b + h:2 * b + h + 1, :], src, "dn", keys_, [])
 
-        def chain(hf, mid, fill):
-            pb = ("B", 2 + hf)
-            ps = T.S1[:, 512 * hf:512 * hf + 32]
-            op("v", lambda: V.tensor_tensor_scan(T.SC[:, hf, :], T.MSK[:], T.S0[:, 512 * hf:512 * hf + 512], 0.0, A.add, A.min),
-               ["MSK"], [("SC", hf), ("B", hf)])
-            key = T.SC[:, hf, 15::16]
-            ts(T.KR[:, hf, :], key, BIG, -BIG, A.add, A.add, [("SC", hf)], [("KR", hf)])
-            cp("v", T.KY[:, hf, :], key, [("SC", hf)], [("KY", hf)])
-            tt(T.CP[:, 2 * hf:2 * hf + 2, 16:32], T.KR[:, hf, :], key, A.is_gt, [("KR", hf), ("SC", hf)], [("CP", hf)])
-            for s in range(8):
-                mm(ps, T.TRI[:] if s == 0 else T.ONE[:], T.CP[:, 2 * hf:2 * hf + 2, 16 - 2 * s:32 - 2 * s], s == 0, s == 7,
-                   ["TRI", "ONE", ("CP", hf)], [pb])
-            mid()
-            ts(T.KO[:, hf, :], T.KY[:, hf, :], 1, 15, A.logical_shift_right, A.bitwise_and, [("KY", hf)], [("KO", hf)])
-            ts(T.KB[:, hf, :], T.KY[:, hf, :], 5, 15, A.logical_shift_right, A.bitwise_and, [("KY", hf)], [("KB", hf)])
-            cp("v", T.OD[:, 64 * hf:64 * hf + 64:2], T.KO[:, hf, :], [("KO", hf)], [("OD", hf)])
-            tt(T.DL[:, hf, :], T.KB[:, hf, :], T.KO[:, hf, :], A.subtract, [("KB", hf), ("KO", hf)], [("DL", hf)])
-            ts(T.GO[:, hf, :], ps, -384.5, None, A.is_lt, None, [], [("GO", hf), pb])
-            tt(T.GD[:, 64 * hf:64 * hf + 64:2], T.GO[:, hf, :], T.DL[:, hf, :], A.mult, [("GO", hf), ("DL", hf)], [("GD", hf)])
-            fill()
-            pt = T.S1[64 * hf:64 * hf + 64, 512 * hf + 128:512 * hf + 256]
-            mm(pt, T.OD[:, 64 * hf:64 * hf + 64], T.IDN[:], True, False, [("OD", hf), "IDN"], [pb])
-            mm(pt, T.GD[:, 64 * hf:64 * hf + 64], T.IDN[:], False, True, [("GD", hf), "IDN"], [pb])
-            return pt
-
-        def turn(e, hf, pt):
-            cp(e, DT[64 * hf:64 * hf + 64, :], pt, [], [("DT", pi, hf), ("B", 2 + hf)])
-
-        def spread_mm(q, k, y):
-            lo = KQ * (32 * q // KQ)
-            for blk in range(4 * y, 4 * y + 4):
-                mm(SL[k][:, 128 * blk:128 * blk + 128], T.SEL[lo:lo + KQ, (8 * q + blk) % NA, :], DT[lo:lo + KQ, :], True, True,
-                   SELK + [("DT", pi, q // 2)], [("B", 2 * k + y)])
-
-        def spread(e, q, k, y):
-            if y is None:
-                sign(e, T.P[:, 2048 * q + pi:2048 * q + 2048:2], k, None, [("P", q, z) for z in range(4)])
+    cutp = T.E3[0:1, 0:2]
+    mm(cutp, T.ACC[64:128, 8:9], T.MW[64:128, :], True, False, [("ACC", 8), "MW"], bk(5))
+    for k in range(4):
+        for a in range(16):
+            c0 = 2048 * k + 128 * a
+            mm(BANK[k][:, 32 * a:32 * a + 32], T.TT[:, c0:c0 + 128], T.CC[:], True, True, TK + [("CC", 0), ("CC", 1)], bk(k))
+        for h in range(2):
+            j = 2 * k + h
+            junk = T.R[:, 512 * j:512 * j + 256]
+            if k == 1:
+                ts(junk, BANK[k][:, h::2], 0.0, None, A.max, None, [], [("R", j)] + bk(k))
             else:
-                c0 = 2048 * q + 1024 * y
-                sign(e, T.P[:, c0 + pi:c0 + 1024:2], k, y, [("P", q, 2 * y), ("P", q, 2 * y + 1)])
-
-        g2("v", 0); g2("a", 2); keys(0); keys(2)
-        g2("v", 1); g2("a", 3); keys(1); keys(3)
-        g2("v", 4); g2("a", 5); g2("a", 6); g2("a", 7)
-        keys(4); keys(5)
-        pa = chain(0, lambda: keys(6), lambda: lists(1) if t == 0 else None)
-        keys(7)
-        if t == 0:
-            op("a", lambda: S.activation(T.Yj[64:128], T.Yw[64:128], F.Identity, accum_out=T.ACC[64:128, 4:5]),
-               [("Yw", q) for q in range(4)], ["Yj", ("ACC", 4)])
-        turn("a", 0, pa)
-        if t == 2:
-            cp("a", T.O[:, 1::2], T.DT1[:], [("DT", 1, 0), ("DT", 1, 1)], ["O1"])
-        spread_mm(0, 2, 0); spread_mm(0, 2, 1); spread_mm(1, 3, 0); spread_mm(1, 3, 1)
-        spread("a", 0, 2, 0); spread("a", 0, 2, 1); spread("a", 1, 3, None)
-        pb_ = chain(1, lambda: None, lambda: None)
-        turn("v", 1, pb_)
-        if t == 2:
-            cp("a", T.O[:, 0::2], T.DT0[:], [("DT", 0, 0), ("DT", 0, 1)], ["O0"])
-        for y in range(2):
-            spread_mm(2, 0, y); spread_mm(3, 2, y)
-        for y in range(2):
-            spread("v", 2, 0, y); spread("a", 3, 2, y)
-
-    for h in range(2):
-        dma("s", T.DO[:, 64 * h:64 * h + 64, :], T.O[2 * h::4, :], "do", ["O0", "O1"], [("DO", h)])
-    for h in range(2):
-        dma("s", T.newpart[2 * me + h:2 * me + h + 1, :], T.O[32 * me + 2 * h:32 * me + 32:4, :], "dn", ["O0", "O1"], [])
-    fused(1, "oa", lambda b: T.DO[b], T.LO[me], [("DO", 0), ("DO", 1)])
-    for b in others:
-        dma("s", T.newpart[2 * b:2 * b + 2, :], T.LO[b], "dn", [("LO", b)], [])
-
-    fb = [(T.S1, 0, 2), (T.S1, 512, 3), (T.S3, 0, 6), (T.S3, 512, 7)]
-    cutp = T.S0[0:1, 0:2]
-
-    def g3(e, c, q):
-        gather_pin(e, 2048 * q + 512 * c, 512, [("TT", q, c)])
-
-    def cnt3(c, qs):
-        buf, c0, bk = fb[c]
-        o = buf[:, c0:c0 + 512]
-        mm(o, T.SWF[0:8, :], T.W[0:8, 512 * c:512 * c + 512], True, False, WK + ["SWF"], [("B", bk)])
-        for q in qs:
-            mm(o, T.Z[:, 96 - 32 * q:224 - 32 * q], T.TT[:, 2048 * q + 512 * c:2048 * q + 512 * c + 512], False, q == qs[-1],
-               ["Z", ("TT", q, c)], [("B", bk)])
-
-    def sum3(c):
-        buf, c0, bk = fb[c]
-        op("a", lambda: S.activation(T.G[:, 512 * c:512 * c + 512], buf[:, c0:c0 + 512], F.Relu, accum_out=T.ACC[:, c:c + 1]),
-           [], [("G", c), ("ACC", c), ("B", bk)])
-
-    for c in range(2):
-        g3("v", c, 0); g3("a", c, 2); g3("v", c, 1); g3("a", c, 3)
-        cnt3(c, [0, 2, 1, 3])
-    sum3(0)
-    g3("v", 2, 0); g3("a", 2, 2); g3("v", 2, 1); g3("a", 2, 3)
-    cnt3(2, [0, 1, 2, 3])
-    sum3(1)
-    g3("v", 3, 0); g3("a", 3, 3); g3("v", 3, 1); g3("v", 3, 2)
-    sum3(2)
-    cnt3(3, [0, 3, 1, 2])
-    sum3(3)
-    mm(cutp, T.ACC[64:128, 4:5], T.MW[64:128, :], True, False, [("ACC", 4), "MW"], [("B", 0)])
-    for c in range(4):
-        mm(cutp, T.ACC[:, c:c + 1], T.MA[:], False, c == 3, [("ACC", c), "MA"], [("B", 0)])
-    cp("v", T.CL[0:1, me, 0:2], cutp, [], ["CLown", ("B", 0)])
+                act(junk, BANK[k][:, h::2], F.Relu, [], [("R", j), ("ACC", j)] + bk(k), accum_out=T.ACC[:, j:j + 1])
+    for j in (2, 3):
+        op("v", lambda: V.tensor_reduce(T.ACC[:, j:j + 1], T.R[:, 512 * j:512 * j + 256], AX.X, A.add), [("R", j)], [("ACC", j)])
+    for k in range(4):
+        mm(cutp, T.NG[:], T.ACC[:, 2 * k:2 * k + 2], False, k == 3, [("ACC", 2 * k), ("ACC", 2 * k + 1), "NG"], bk(5))
+    cp("v", T.CL[0:1, me, 0:2], cutp, [], ["CLown"] + bk(5))
     deps("g", ["CLown"], [])
     en = [e for x in share(me, 0).values() for e in x]
     g.remote_dma_fused([RemoteDMATransfer(dst_ids=[dst(b) for b in others], dma_engine_mask=bits(en), remote_sem=T.sem.ca,
                                           srcs=[T.CL[:, me, :]], dsts=[T.CL[:, me, :] for b in others])], local_sem=T.sem.sent)
     cnt["sent"] += len(en)
-    dma("s", T.cut[:], T.CL[0:1, :, 0:2], "dc", ["CLown", "CLfar"], [])
+    dma("a", T.cut[:], T.CL[0:1, :, 0:2], "dc", ["CLown", "CLfar"], [])
 
     for s in SEMAPHORES:
         if cnt[s] > waited[s]:

@@ -4,8 +4,10 @@ from concourse.mybir import AluOpType as A, ActivationFunctionType as F, AxisLis
 R2048, R128, R32 = 1.5 * 2.0 ** 34, 1.5 * 2.0 ** 30, 1.5 * 2.0 ** 28
 WIN = 8192 + 512
 SEED = WIN // 16
+CUT = [32, 30, 30, 30]
+WHEN = [12, 18, 18]
+PIECES = [(12, "aa"), (12, "vv"), (16, "aa"), (10, "vv"), (14, "aa")]
 SCRATCH = {
-    "DY": ("dram", [4, 128, 64], "int32"),
     "DI": ("dram", [4, 128, 128], "int32"),
     "KS": ("psum", [128, 1024], "float32"),
     "E0": ("psum", [128, 512], "float32"),
@@ -13,28 +15,29 @@ SCRATCH = {
     "E2": ("psum", [128, 512], "float32"),
     "E3": ("psum", [128, 512], "float32"),
     "E4": ("psum", [128, 32, 16], "float32"),
-    "PM": ("psum", [128, 6, 72], "float32"),
+    "PM": ("psum", [128, 7, 72], "float32"),
 }
 for _names, _shape, _dt in [
-        ("Y", [4, 64], "int32"), ("Yb Yw Yj", [4, 64], "bfloat16"), ("W", [2048], "bfloat16"),
+        ("YI", [256], "int32"), ("Y Yw Yj", [4, 128], "bfloat16"), ("W", [2048], "bfloat16"),
         ("S32 NL", [4, 128], "int32"), ("S16 PL", [512], "uint16"), ("IL", [2, 256], "uint16"),
-        ("OFF", [32], "uint16"), ("P R", [8192], "bfloat16"), ("TT WT", [WIN], "bfloat16"), ("G P2", [4096], "bfloat16"),
-        ("MX", [4, 128], "float32"), ("KI", [4], "int32"), ("CI", [8], "int32"), ("CF", [24], "float32"), ("J32", [36], "float32"),
-        ("JP JH B1 B2 EI EA EB", [32], "float32"), ("NE MZ", [4], "float32"),
-        ("BI C C2 ONE IDN NID TRI SH BD NBD D512 PERM IOTA OS BT DT DNZ RS S0", [128], "bfloat16"),
-        ("SELI", [32, 128], "bfloat16"), ("SW SELD", [4, 128], "bfloat16"), ("U", [8, 128], "bfloat16"),
-        ("Z R1 R2 MK8", [32], "bfloat16"), ("CC", [16, 2], "bfloat16"), ("SP", [8, 16], "bfloat16"), ("SQ", [2, 16], "bfloat16"),
+        ("OFF", [32], "uint16"), ("P R", [8192], "bfloat16"), ("TT WT", [WIN], "bfloat16"), ("G", [4096], "bfloat16"), ("P2", [2048], "bfloat16"),
+        ("MX", [4, 8, 2, 8], "float32"), ("KI", [4], "int32"), ("CI", [4], "int32"), ("CF", [8], "float32"),
+        ("J32 EI", [32], "float32"), ("EJ", [16], "float32"), ("NE MZ", [4], "float32"),
+        ("JH HM C C2 ONE IDN NID TRI SH BD NBD D512 PERM IOTA OS BT DT DNZ REP S0", [128], "bfloat16"),
+        ("SELI", [16, 128], "bfloat16"), ("SELD", [4, 128], "bfloat16"), ("U", [8, 128], "bfloat16"),
+        ("Z0 Z KT R1 R2 MK8", [32], "bfloat16"), ("CC", [16, 2], "bfloat16"), ("SP", [2, 8, 16], "bfloat16"), ("RS", [2, 128], "bfloat16"),
         ("DS DG", [512], "bfloat16"), ("KC", [256], "bfloat16"), ("ZR", [288], "bfloat16"),
         ("MSK", [256], "float32"), ("MW", [2], "float32"), ("NG", [1], "float32"),
         ("SC", [1024], "float32"), ("KR ZZ", [64], "float32"), ("NS", [72], "float32"),
-        ("FF LL TL BB OWN BST GO DL GD", [64], "bfloat16"), ("SB", [88], "bfloat16"), ("SI TM", [288], "float32"),
-        ("ST", [128], "float32"), ("X32", [4, 132], "float32"), ("MD", [4, 8, 9], "float32"), ("OM", [6, 8, 9], "bfloat16"),
-        ("M1", [2, 6, 8, 9], "bfloat16"), ("M2", [2, 4, 8, 9], "bfloat16"),
+        ("FF LL TL BB OWN BST GO DL GD", [64], "bfloat16"), ("NB", [2, 2, 16], "bfloat16"), ("SB", [160], "bfloat16"),
+        ("SI TM", [288], "float32"), ("ST", [128], "float32"), ("X32", [4, 132], "float32"), ("MD", [4, 8, 9], "float32"),
+        ("OM", [7, 8, 9], "bfloat16"), ("M1", [2, 7, 8, 9], "bfloat16"), ("WL", [2, 64], "uint16"), ("GW", [1024], "bfloat16"),
+        ("SW", [8], "bfloat16"), ("WV", [64], "bfloat16"), ("M2", [2, 4, 8, 9], "bfloat16"),
         ("NPO LO", [4, 2, 16], "float32"), ("ACC", [12], "float32"), ("CL", [4, 4], "float32")]:
     for _n in _names.split():
         SCRATCH[_n] = ("sbuf", [128] + _shape, _dt)
-SEMAPHORES = (["ev", "ea", "et", "eg", "dy", "dyo", "dp", "di", "dio", "dt", "w1", "w2", "w3", "dn", "dc", "ca", "sent"]
-              + ["%s%d" % (n, q) for n in ("ya", "pa", "ia", "oa", "dw") for q in range(4)])
+SEMAPHORES = (["ev", "ea", "et", "eg", "dy", "dyw", "dp", "di", "dio", "dw", "dt", "w1", "w2", "w3", "w4", "wl", "dn", "dc", "ca", "sy", "sent"]
+              + ["%s%d" % (n, q) for n in ("ya", "wa", "pa", "ia", "oa") for q in range(4)])
 
 
 def rank_program(g, core, T, topo):
@@ -119,11 +122,14 @@ def rank_program(g, core, T, topo):
         else:
             act(out, in_, F.Copy, reads, writes)
 
+    def scaled(e, out, in_, c, reads, writes):
+        if e == "a":
+            act(out, in_, F.Identity, reads, writes, scale=c)
+        else:
+            ts(out, in_, c, None, A.mult, None, reads, writes)
+
     def mm(out, l, r, st, sp, reads, writes):
         op("t", lambda: PE.matmul(out, l, r, st, sp), reads, writes)
-
-    def ms(ap, c, writes):
-        op("v", lambda: V.memset(ap, c), [], writes)
 
     def io(out, pat, base, cm, writes, flag=True):
         if flag:
@@ -134,6 +140,9 @@ def rank_program(g, core, T, topo):
     def af(out, in_, pat, cmp, fill, base, cm, reads, writes):
         op("g", lambda: g.affine_select(out, in_, pat, cmp, fill, base, cm), reads + ["POOL"], writes)
 
+    def put_in(ap, pat, fill, base, key):
+        af(ap, ap, pat, A.not_equal, fill, base, 1, [], [key])
+
     def hops(a, b):
         ca, cb = topo.chip(cores[a]), topo.chip(cores[b])
         return 0 if ca == cb else 1 if topo.mates(ca, cb) else 2 if topo.same_plane(ca, cb) else 3
@@ -141,12 +150,15 @@ def rank_program(g, core, T, topo):
     def peers(a):
         return sorted([b for b in range(n) if b != a], key=lambda b: (hops(a, b), b))
 
-    def share(a, turn):
+    def engines(a):
         ps = peers(a)
-        en = [e for e in topo.engines(cores[a], cores[ps[0]]) if all(e in topo.engines(cores[a], cores[b]) for b in ps)]
+        return [e for e in topo.engines(cores[a], cores[ps[0]]) if all(e in topo.engines(cores[a], cores[b]) for b in ps)]
+
+    def share(a, turn):
+        en = engines(a)
         k = len(en) // 4
         cuts = [en[:2 * k], en[2 * k:3 * k], en[3 * k:4 * k]]
-        return dict((b, cuts[(j + turn) % 3]) for j, b in enumerate(ps))
+        return dict((b, cuts[(j + turn) % 3]) for j, b in enumerate(peers(a)))
 
     def bits(en):
         return sum(1 << e for e in en)
@@ -163,81 +175,61 @@ def rank_program(g, core, T, topo):
                             for b in others], local_sem=T.sem.sent)
         cnt["sent"] += sum(len(sh[b]) for b in others)
 
+    def to_all(sem, ap, reads, left="sent"):
+        deps("g", reads, [])
+        g.remote_dma_fused([RemoteDMATransfer(dst_ids=[dst(b) for b in others], dma_engine_mask=bits(engines(me)), remote_sem=sem,
+                                              srcs=[ap], dsts=[ap for b in others])], local_sem=T.sem[left])
+        lands(left, left, len(engines(me)))
+
     others = peers(me)
     order = [me] + others
     for b in others:
-        lands(("Y", b), "ya%d" % b, len(topo.engines(cores[b], core)))
+        lands(("Y", b), "ya%d" % b, len(engines(b)))
+        lands(("Yw", b), "wa%d" % b, len(engines(b)))
         lands(("PL", b), "pa%d" % b, len(share(b, 0)[me]))
         lands(("NL", b), "ia%d" % b, len(share(b, 1)[me]))
         lands(("LO", b), "oa%d" % b, len(share(b, 1)[me]))
-        lands("CLfar", "ca", sum(len(x) for x in share(b, 0).values()))
+        lands("CLfar", "ca", len(engines(b)))
 
-    dma("s", T.DY[:, 0:64, :], T.part[:], "dy", [], [("DY", 0)])
-    dma("a", T.DY[:, 64:128, :], T.w[:], "dy", [], [("DY", 1)])
-    DYK = [("DY", 0), ("DY", 1)]
-    dma("s", T.Y[0:64, me, :], T.part[2 * me:2 * me + 2, :], "dyo", [], [("Y", me)])
-    dma("a", T.Y[64:128, me, :], T.w[2 * me:2 * me + 2, :], "dyo", [], ["Yown"])
+    dma("s", T.YI[:, 0:128], T.part[:], "dy", [], [("YI", 0)])
+    dma("s", T.YI[:, 128:256], T.w[:], "dyw", [], [("YI", 1)])
     for r in range(4):
         for i in range(4):
             dma("sa"[i // 2], T.S32[32 * i:32 * i + 32, r, :], T.pin[32 * r:32 * r + 32, 128 * i:128 * i + 128], "dp", [], [("S32", r, i)])
     S32K = [("S32", r, i) for r in range(4) for i in range(4)]
+    dma("s", T.DI[:], T.inc[:], "di", [], ["DI"])
+    mine = slice(32 * me, 32 * me + 32)
 
     io(T.KI[:, 0:1], [[0, 1]], 0, 1, ["KI"], False)
-    io(T.J32[:], [[1, 36]], 0, 0, ["J32"])
-    io(T.JH[:], [[1, 2], [0, 16]], 0, 0, ["JH"])
-    io(T.JP[:], [[0, 2], [1, 16]], 0, 0, ["JP"])
+    io(T.J32[:], [[1, 32]], 0, 0, ["J32"])
+    io(T.JH[:], [[0, 4], [1, 2], [0, 16]], 0, 0, ["JH"])
+    io(T.Z0[0:32, :], [[0, 32]], 0, 0, ["Z0"])
     io(T.ONE[:], [[0, 128]], 1, 0, ["ONE"])
-    io(T.IOTA[:], [[1, 128]], 0, 0, ["IOTA"])
-    io(T.CF[:, 16:17], [[0, 1]], 1, 1, ["c16"])
-    deps("g", DYK, [])
-    for b in others:
-        rid, pid, _e = topo.addr(cores[b])
-        g.remote_dma(T.Y[:, me, :], T.DY[b], T.sem["ya%d" % me], T.sem.sent, pid, rid, topo.mask(core, cores[b]))
-        cnt["sent"] += len(topo.engines(core, cores[b]))
+    z = T.Z0[0:32, :]
+    put_in(z, [[-1, 32]], -16.0, -1, "Z0")
+    af(T.REP[0:32, :], T.ONE[0:32, :], [[0, 4], [-1, 32]], A.is_equal, 0.0, 0, 1, ["ONE"], ["REP"])
+    put_in(z, [[-1, 32]], -16.0, 1, "Z0")
+    put_in(z, [[-1, 32]], 32.0, 0, "Z0")
 
-    for j, (sh_, an) in enumerate([(0, 31), (5, 3), (0, 15)]):
+    for j, (sh_, an) in enumerate([(0, 15), (4, 1), (0, 31), (5, 3)]):
         ts(T.CI[:, j:j + 1], T.KI[:, 0:1], sh_, an, A.logical_shift_right, A.bitwise_and, ["KI"], [("CI", j)])
-    ms(T.Yb[64:128], 1.0, ["Yb1"])
-    cp("v", T.CF[:, 0:3], T.CI[:, 0:3], [("CI", j) for j in range(3)], ["CF"])
+    cp("v", T.CF[:, 0:4], T.CI[:], [("CI", j) for j in range(4)], ["CF"])
 
     def col(j):
         return T.CF[:, j:j + 1]
-
-    def scaled(e, out, in_, c, reads, writes):
-        if e == "a":
-            act(out, in_, F.Identity, reads, writes, scale=c)
-        else:
-            ts(out, in_, c, None, A.mult, None, reads, writes)
-    ts(col(14), col(1), 2.0, None, A.is_equal, None, ["CF"], ["c14"])
-    ts(col(15), col(1), 2.0, -2.0, A.is_equal, A.mult, ["CF"], ["c15"])
-    ts(T.EI[:], T.J32[:, 0:32], col(0), None, A.is_equal, None, ["J32", "CF"], ["EI"])
-    ts(T.B1[:], T.JH[:], col(1), 2.0, A.is_equal, A.mult, ["JH", "CF"], ["B1"])
-    ts(T.B2[:], T.JP[:], col(15), col(14), A.mult, A.add, ["JP", "c14", "c15"], ["B2"])
-    ts(col(11), col(2), 0.0, None, A.is_equal, None, ["CF"], ["c11"])
-    for i in range(4):
-        tt(T.BI[:, 32 * i:32 * i + 32], T.B1[:], T.B2[:], A.add, ["B1", "B2"], [("BI", i)])
-    for a in range(32):
-        scaled("a" if a % 5 in (1, 3) else "v", T.SELI[:, a, :], T.BI[:], T.EI[:, a:a + 1],
-               [("BI", i) for i in range(4)] + ["EI"], [("SELI", a)])
-    CK = [("C", i) for i in range(4)]
-
-    def pins():
-        cp("v", T.S16[:], T.S32[:], S32K, ["S16"])
-        fused(0, "pa", lambda b: T.S16[:, 128 * b:128 * b + 128], T.PL[:, 128 * me:128 * me + 128], ["S16"])
-
-    def more():
-        ts(col(12), col(11), 16.0, col(0), A.mult, A.add, ["c11", "CF"], ["c12"])
-        ts(col(13), col(11), -16.0, 8.0, A.mult, A.add, ["c11"], ["c13"])
-        scaled("a", T.EA[:], T.EI[:], -8.0, ["EI"], ["EA"])
-        ts(T.NE[:], T.J32[:, 0:4], col(1), None, A.not_equal, None, ["J32", "CF"], ["NE"])
-        ts(T.EB[:], T.J32[:, 1:33], col(12), col(13), A.is_equal, A.mult, ["J32", "c12", "c13"], ["EB"])
-        cp("v", T.PL[:, 128 * me:128 * me + 128], T.S16[:, 128 * me:128 * me + 128], ["S16"], [("PL", me)])
-        tt(T.Z[:], T.EA[:], T.EB[:], A.add, ["EA", "EB"], ["Z"])
-        ts(T.MZ[:], T.J32[:, 0:4], col(1), None, A.is_equal, None, ["J32", "CF"], ["MZ"])
-        ts(T.MW[:], T.J32[:, 2:4], col(1), 15.0, A.is_equal, A.mult, ["J32", "CF"], ["MW"])
-        scaled("a", T.R1[:], T.EI[:], 2048.0, ["EI"], ["R1"])
-        for i in range(4):
-            scaled("a", T.C[:, 32 * i:32 * i + 32], T.Z[:], T.NE[:, i:i + 1], ["Z", "NE"], [("C", i)])
+    ts(T.EJ[:], T.J32[:, 0:16], col(0), None, A.is_equal, None, ["J32", "CF"], ["EJ"])
+    ts(T.HM[:], T.JH[:], col(1), None, A.is_equal, None, ["JH", "CF"], ["HM"])
+    BIAS = col(4)
+    ts(BIAS, T.EJ[:, 15:16], 16.0, col(0), A.mult, A.subtract, ["EJ", "CF"], ["BIAS"])
+    for a in range(16):
+        scaled("va"[a % 2], T.SELI[:, a, :], T.HM[:], T.EJ[:, a:a + 1], ["HM", "EJ"], [("SELI", a)])
+        if a == 10:
+            cp("v", T.Y[:, me, :], T.YI[:, 0:128], [("YI", 0)], [("Y", me)])
+            cp("v", T.Yw[:, me, :], T.YI[:, 128:256], [("YI", 1)], [("Yw", me)])
+    to_all(T.sem["ya%d" % me], T.Y[:, me, :], [("Y", me)])
+    to_all(T.sem["wa%d" % me], T.Yw[:, me, :], [("Yw", me)])
+    ts(T.EI[:], T.J32[:], col(2), None, A.is_equal, None, ["J32", "CF"], ["EI"])
+    ts(T.MZ[:], T.J32[:, 0:4], col(3), None, A.is_equal, None, ["J32", "CF"], ["MZ"])
 
     BANK = [T.KS[:, 0:512], T.KS[:, 512:1024], T.E0[:], T.E1[:], T.E2[:], T.E3[:], T.E4[:]]
     TURN = [0, 1, 2, 3, 4, 6]
@@ -248,54 +240,48 @@ def rank_program(g, core, T, topo):
     def part(k, a, b):
         return T.E4[:, a // 16:b // 16, :] if k == 6 else T.PM[:, a // 64:b // 64, 0:64] if k == 7 else BANK[k][:, a:b]
 
-    def sign(q, out, k, writes):
-        if q == "v":
-            ts(out, BANK[k], -1.0, 1.0, A.max, A.min, [], writes + bk(k))
+    def ramp(e, out, k, writes):
+        if e == "v":
+            ts(out, BANK[k], BIAS, 0.0, A.add, A.max, ["BIAS"], writes + bk(k))
         else:
-            act(out, BANK[k], F.Sign, [], writes + bk(k))
+            act(out, BANK[k], F.Relu, ["BIAS"], writes + bk(k), bias=BIAS)
 
     PK = [("P", c) for c in range(16)]
-    RK = [("R", c) for c in range(16)]
-    TK = [("TT", c) for c in range(16)]
-
-    def narrow(j):
-        q = order[j]
-        cp("v", T.Yb[0:64, q, :], T.Y[0:64, q, :], [("Y", q)], [("Yb", q)])
+    RK = [("R", c) for c in range(32)]
+    TK = [("TT", c) for c in range(32)]
+    CK = [("C", i) for i in range(4)]
 
     def take(j):
         q = order[j]
-        if j < 2:
-            narrow(j)
         for y in range(4):
             k = (4 * j + y) % 7
-            for al in range(8 * y, 8 * y + 8):
-                c0 = 64 * (al % 8)
-                mm(part(k, c0, c0 + 64), T.SELI[0:96, al, :], T.Yb[0:96, q, :], True, True,
-                   [("SELI", al), ("Yb", q), "Yb1"], bk(k))
-            if y == 0:
-                cp("v", T.Yw[64:128, q, :], T.Y[64:128, q, :], [("Y", q), "Yown"], [("Yw", q)])
-            if y == 3 and j in (1, 2):
-                narrow(j + 1)
-            if j > 0:
-                put(j, y)
+            for a in range(4 * y, 4 * y + 4):
+                c0 = 128 * (a % 4)
+                mm(part(k, c0, c0 + 128), T.SELI[mine, a, :], T.Y[mine, q, :], True, True, [("SELI", a), ("Y", q)], bk(k))
+            ramp("av"[y % 2], T.P[:, 2048 * q + 512 * y:2048 * q + 512 * y + 512], k, [("P", 4 * q + y)])
+
+    take(0)
+    cp("v", T.S16[:], T.S32[:], S32K, ["S16"])
+    af(z, z, [[-16, 2], [0, 16]], A.is_ge, 0.0, 0, 1, [], ["Z0"])
+    io(T.KT[:], [[0, 2], [2, 16]], 66, 0, ["KT"])
+    af(z, z, [[16, 2], [0, 16]], A.is_ge, 0.0, 14, -1, [], ["Z0"])
+    put_in(T.Z0[0:32, 0::16], [[-16, 2]], -16.0, -15, "Z0")
+    fused(0, "pa", lambda b: T.S16[:, 128 * b:128 * b + 128], T.PL[:, 128 * me:128 * me + 128], ["S16"])
+    fused(1, "ia", lambda b: T.DI[b], T.NL[:, me], ["DI"])
+    cp("v", T.PL[:, 128 * me:128 * me + 128], T.S16[:, 128 * me:128 * me + 128], ["S16"], [("PL", me)])
+    act(T.NE[:], T.MZ[:], F.Identity, ["MZ"], ["NE"], scale=-1.0, bias=1.0)
+    scaled("a", T.R1[:], T.EI[:], 2048.0, ["EI"], ["R1"])
+    mm(T.PM[:, 0, 0:32], T.REP[0:32, :], z, True, True, ["REP", "Z0"], bk(7))
+    cp("v", T.Z[:], T.PM[:, 0, 0:32], [], ["Z"] + bk(7))
+    tt(T.R2[:], T.PM[:, 0, 0:32], T.KT[:], A.mult, ["KT"], ["R2"] + bk(7))
+    for i in range(4):
+        scaled("av"[i % 2], T.C[:, 32 * i:32 * i + 32], T.Z[:], T.NE[:, i:i + 1], ["NE", "Z"], [("C", i)])
+    take(1); take(2); take(3)
+    dma("s", T.NL[:, me, :], T.inc[mine, :], "dio", [("Y", others[0])], [("NL", me)])
+    NLK = [("NL", q) for q in range(4)]
+    for q in order:
         for h in range(2):
-            dma("s", T.W[2 * q + h:2 * q + h + 1, :], T.Yw[64 + 32 * h:96 + 32 * h, q, :], "dw%d" % q, [("Yw", q)], [("W", q, h)])
-
-    def put(j, y):
-        q = order[j]
-        sign("av"[y % 2], T.P[:, 2048 * q + 512 * y:2048 * q + 512 * y + 512], (4 * j + y) % 7, [("P", 4 * q + y)])
-
-    take(0); pins()
-    for y in range(4):
-        put(0, y)
-    more()
-    take(1)
-    for i in range(4):
-        dma("s", T.DI[:, 32 * i:32 * i + 32, :], T.inc[:, 128 * i:128 * i + 128], "di", [], [("DI", i)])
-    take(2); take(3)
-    for i in range(4):
-        dma("s", T.NL[32 * i:32 * i + 32, me, :], T.inc[32 * me:32 * me + 32, 128 * i:128 * i + 128], "dio", [], [("NL", me, i)])
-    NLK = [("NL", q) for q in others] + [("NL", me, i) for i in range(4)]
+            dma("s", T.W[2 * q + h:2 * q + h + 1, :], T.Yw[32 * me + 16 * h:32 * me + 16 * h + 16, q, :], "dw", [("Yw", q)], [("W", q, h)])
     WK = [("W", q, h) for q in range(4) for h in range(2)]
 
     def diag(out, base, fill, key, src=None):
@@ -303,64 +289,57 @@ def rank_program(g, core, T, topo):
             af(out, T.ONE[:], [[-1, 128]], A.is_equal, 0.0, base, 1, ["ONE"], [key])
         else:
             af(out, T[src][:], [[-1, 128]], A.not_equal, fill, base, 1, [src], [key])
-    for q in order:
-        af(T.SW[0:8, q, :], T.ONE[0:8, :], [[0, 4], [-1, 2], [0, 16]], A.is_equal, 0.0, -2 * q, 1, ["ONE"], [("SW", q)])
-    io(T.ST[:], [[0, 128]], 1, 0, [("ST", z) for z in range(4)])
+    io(T.MX[:], [[0, 512]], 0, 0, [("MX", j) for j in range(4)])
     io(T.MD[:, 0:2], [[0, 144]], 0, 0, [("MD", 0), ("MD", 1)])
     io(T.WT[:, 0:SEED], [[0, SEED]], 1, 0, [("WT", 0)])
+    row = [[-1, 4], [-64, 2], [-8, 8]]
     for j in range(4):
-        af(T.MX[:, j, :], T.ST[:], [[-16, 8], [1000, 2], [-2, 8]], A.is_equal, 0.0, -(j // 2) - 1000 * (j % 2), 1,
-           [("ST", 0)], [("MX", j)])
-    fused(1, "ia", lambda b: T.DI[b], T.NL[:, me], [("DI", i) for i in range(4)])
+        put_in(T.MX[:, j, :, j % 2, :], row, 1.0, -4 * (j // 2), ("MX", j))
     for x in range(2):
         for pi in range(2):
-            v_ = T.MD[:, pi, :, 1 - x:9 - x]
-            af(v_, v_, [[-16, 8], [-2, 8]], A.not_equal, 1.0 - 2 * x, -pi, 1, [("MD", pi)], [("MD", pi)])
+            put_in(T.MD[:, pi, :, 1 - x:9 - x], row, 1.0 - 2 * x, -4 * pi, ("MD", pi))
     io(T.X32[:, :, 0], [[0, 4]], 0, 0, ["X0"])
     io(T.ZR[0:1, :], [[0, 288]], 0, 0, ["ZR"])
-    hp = [[-16, 2], [0, 16]]
-    r2 = [T.R2[32 * j:32 * j + 32, :] for j in range(4)]
-    io(T.R2[0:64, :], [[0, 32]], 0, 0, [("R2", 0), ("R2", 1)])
-    af(r2[0], r2[0], [[16, 2], [0, 16]], A.is_ge, 0.5, 0, -1, [], [("R2", 0)])
     io(T.KC[0:1, :], [[0, 16], [32, 16]], 1056, 0, ["KC"])
-    af(r2[0], r2[0], [[16, 2], [0, 16]], A.is_ge, 0.0, 15, -1, [], [("R2", 0)])
-    io(r2[2], [[0, 2], [-16, 16]], -528, 0, [("R2", 2), "POOL"])
-    io(r2[3], [[0, 2], [16, 16]], 528, 0, [("R2", 3), "POOL"])
-    af(r2[1], r2[1], hp, A.not_equal, 7.5, 0, 1, [], [("R2", 1), "POOL"])
-    af(r2[2], r2[2], [[-1, 32]], A.is_equal, 0.0, 0, 1, [], [("R2", 2), "POOL"])
-    af(r2[3], r2[3], [[-1, 32]], A.is_equal, 0.0, -1, 1, [], [("R2", 3), "POOL"])
-    last = T.R2[96:128, 15::16]
-    io(last, [[0, 2]], -768, 0, [("R2", 3), "POOL"])
-    af(last, last, [[-16, 2]], A.is_equal, 0.0, 0, 1, [], [("R2", 3), "POOL"])
-    R2K = [("R2", j) for j in range(4)]
+    for x in (32, 96):
+        af(T.R2[x:x + 32, :], T.ONE[x:x + 32, 0:32], [[-16, 2], [0, 16]], A.is_equal, 0.0, 0, 1, ["ONE"], ["R2", "POOL"])
+    R2K = ["R2"]
     io(T.MSK[:], [[0, 256]], 0, 0, ["MSK"])
     diag(T.IDN[:], 0, None, "IDN")
     io(T.MSK[:, 0::16], [[0, 16]], 262144, 0, ["MSK"])
-    io(T.OM[0:2], [[0, 432]], 0, 0, ["OM"])
+    io(T.OM[0:2], [[0, 504]], 0, 0, ["OM"])
     io(T.OS[0:2, :], [[1, 128]], 0, 0, ["OS"])
-    io(T.OM[0:2, 2:6, :, 0], [[0, 8], [128, 4]], 8192, 0, ["OM"])
-    af(T.OS[0:2, :], T.OS[0:2, :], [[0, 128]], A.is_equal, 1.0, 0, 1, ["OS"], ["OS"])
-    af(T.OM[0:2, 2:6, :, 0], T.OM[0:2, 2:6, :, 0], [[0, 32]], A.not_equal, 1.0, 0, 1, ["OM"], ["OM"])
+    io(T.OM[0:2, 3:7, :, 0], [[0, 8], [128, 4]], 8192, 0, ["OM"])
+    put_in(T.OS[0:2, :], [[0, 128]], 1.0, -1, "OS")
+    put_in(T.OM[0:2, 3:7, :, 0], [[0, 32]], 1.0, 0, "OM")
     af(T.MK8[:], T.ONE[:, 0:32], [[0, 4], [1, 8]], A.not_equal, 0.0, 0, 0, ["ONE"], ["MK8"])
     io(T.OM[0:2, 0, :, 0], [[0, 8]], 1, 0, ["OM"])
     af(T.TRI[:], T.ONE[:], [[1, 128]], A.is_gt, 0.0, 0, -1, ["ONE"], ["TRI"])
     diag(T.SH[:], 1, None, "SH")
+    io(T.IOTA[:], [[1, 128]], 0, 0, ["IOTA"])
     diag(T.BD[:], 1, -1.0, "BD", "IDN")
     diag(T.NBD[:], 0, -1.0, "NBD", "SH")
     diag(T.D512[:], 0, -512.0, "D512", "IDN")
-    io(T.S0[0:9, :], [[0, 8], [-32, 16]], 1008, 0, ["S0"])
+    NEXT = col(5)
+    io(NEXT, [[0, 1]], 1, 1, ["NEXT"])
+    io(T.S0[0:17, :], [[0, 128]], 31, 0, ["S0"])
     af(T.PERM[:], T.ONE[:], [[-1, 32], [-32, 4]], A.is_equal, 0.0, 0, 1, ["ONE"], ["PERM"])
-    af(T.S0[0:9, :], T.S0[0:9, :], [[0, 128]], A.is_equal, 0.0, 0, 1, ["S0"], ["S0"])
-    io(T.SB[:, 8:9], [[0, 1]], 1, 0, ["SB0"])
+    af(T.S0[0:17, :], T.S0[0:17, :], [[0, 128]], A.is_equal, 0.0, 0, 1, [], ["S0"])
+    io(T.SB[:, 8:153:9], [[0, 17]], 1, 0, ["SB", "SBw"])
     for q in range(4):
-        af(T.SELD[0:9, q, :], T.S0[0:9, :], [[0, 4], [-4, 2], [0, 16]], A.not_equal, 1.0, -1 - q, 1, ["S0"], [("SELD", q)])
-    io(T.DT[64:96, :], [[0, 128]], 1, 0, ["DT1", "POOL"])
-    af(T.DNZ[:], T.IDN[:], [[0, 8], [1, 16]], A.not_equal, 0.0, 0, 0, ["IDN"], ["DNZ"])
-    af(T.RS[0:4, :], T.ONE[0:4, :], [[-1, 128]], A.is_equal, 0.0, 0, 16, ["ONE"], ["RS"])
-    af(T.SP[0:4], T.ONE[0:4, :], [[0, 4], [-1, 2], [0, 16]], A.is_equal, 0.0, 0, 1, ["ONE"], ["SP"])
-    af(T.SQ[0:4], T.ONE[0:4, 0:32], [[-1, 2], [0, 16]], A.is_equal, 0.0, 0, 1, ["ONE"], ["SQ"])
-    af(T.SP[0:4, :, 0::15], T.SP[0:4, :, 0::15], [[0, 4], [-1, 2], [0, 2]], A.not_equal, -24.0, -2, 1, ["SP"], ["SP"])
-    af(T.SQ[0:4, :, 0::15], T.SQ[0:4, :, 0::15], [[-1, 2], [0, 2]], A.not_equal, -32.0, -2, 1, ["SQ"], ["SQ"])
+        af(T.SELD[0:17, q, :], T.S0[0:17, :], [[0, 4], [-4, 2], [0, 16]], A.not_equal, 1.0 / 32, -1 - q, 1, ["S0"], [("SELD", q)])
+    SELDK = [("SELD", q) for q in range(4)]
+    io(T.SELD[0:17, :, 15:32:16], [[0, 8]], 0, 0, SELDK)
+    af(T.SW[:], T.ONE[:, 0:8], [[-16, 2], [-32, 4]], A.is_equal, 0.0, -15, 1, ["ONE"], ["SW"])
+    for pat, fill, base in (([[-1, 4], [-4, 2]], 1.0, -9), ([[0, 8]], -1.0, 0)):
+        af(T.SELD[0:17, :, 15:32:16], T.SELD[0:17, :, 15:32:16], pat, A.not_equal, fill, base, 1, [], SELDK)
+    af(T.DNZ[:], T.IDN[:], [[16, 8], [-100, 16]], A.is_gt, 0.0, 1484, 0, ["IDN"], ["DNZ"])
+    for s_ in range(2):
+        af(T.RS[0:4, s_, :], T.ONE[0:4, :], [[-1, 128]], A.is_equal, 0.0, 15 * s_, 16, ["ONE"], [("RS", s_)])
+    io(T.SP[0:4, 0], [[0, 128]], 0, 0, [("SP", 0)])
+    af(T.SP[0:4, 1], T.ONE[0:4, :], [[0, 4], [-1, 2], [0, 16]], A.is_equal, 0.0, 0, 1, ["ONE"], [("SP", 1)])
+    for s_, fill, base in ((0, -16.0, 0), (1, -16.0, -2), (0, 16.0, -2)):
+        put_in(T.SP[0:4, s_, 2:8, 0], [[0, 3], [-1, 2]], fill, base, ("SP", s_))
     io(T.NG[:], [[0, 1]], -1, 0, ["NG"])
     io(T.CL[:, me, :], [[0, 4]], 0, 0, ["CLown"])
 
@@ -370,10 +349,10 @@ def rank_program(g, core, T, topo):
         dma("s", T.WT[:, 4 * SEED * j:4 * SEED * (j + 1)], T.WT[:, 0:4 * SEED], "w2", [("WT", x) for x in range(4)], [("WT", 3 + j)])
     WTK = [("WT", x) for x in range(7)]
     for h in range(2):
-        dma("s", T.WT[16 * h:16 * h + 1, 0:8192], T.W[h:8:2, :], "w3", WK, WTK if h == 0 else ["WTb"])
+        dma("s", T.WT[16 * h + 15:16 * h + 16, 0:8192], T.W[h:8:2, :], "w3", WK, WTK if h == 0 else ["WTb"])
 
     def lists_mm(pi, k, x):
-        mm(part(k, 0, 256), T.MX[:, 2 * pi + x, :], T.X32[:, :, 1 + x:129:2], x == 0, x == 1, [("MX", 2 * pi + x), "X32"], bk(k))
+        mm(part(k, 0, 256), T.MX[:, 2 * pi + x], T.X32[:, :, 1 + x:129:2], x == 0, x == 1, [("MX", 2 * pi + x), "X32"], bk(k))
 
     def lists(pi, k):
         cp("v", T.IL[:, pi], part(k, 0, 256), [], [("IL", pi)] + bk(k))
@@ -392,59 +371,74 @@ def rank_program(g, core, T, topo):
 
     def steps_high(pi):
         act(T.TM[:], T.E3[:, 0:288], F.Identity, [], ["TM"] + bk(5), bias=R128)
-        steps_mm(pi, range(4), False)
         for q in range(4):
-            act(T.M1[:, pi, 2:6, q::4, :], T.TM[:, 72 * q:72 * q + 72], F.Identity, ["TM"], [("M1", pi, q)], bias=-R128)
-        for q in range(4):
-            mm(T.E3[:, 72 * q:72 * q + 72], T.NID[:], T.M1[:, pi, 2:6, q::4, :], False, q == 3, ["NID", ("M1", pi, q)], bk(5))
+            act(T.M1[:, pi, 3:7, q::4, :], T.TM[:, 72 * q:72 * q + 72], F.Identity, ["TM"], [("M1", pi, q)], bias=-R128)
+
+    def steps_again(pi, qs):
+        steps_mm(pi, qs, False)
+        for q in qs:
+            mm(T.E3[:, 72 * q:72 * q + 72], T.NID[:], T.M1[:, pi, 3:7, q::4, :], False, q == 3, ["NID", ("M1", pi, q)], bk(5))
 
     def steps_low(pi):
         for q in range(4):
             cp("a", T.M2[:, pi, :, q::4, :], T.E3[:, 72 * q:72 * q + 72], [], [("M2", pi, q)] + bk(5))
 
-    def relu(e, c, k):
-        o = T.R[:, 512 * c:512 * c + 512]
+    def relu(e, a, b, k):
+        keys_ = [("R", c) for c in range(a // 256, b // 256)] + bk(k)
         if e == "v":
-            ts(o, BANK[k], 0.0, None, A.max, None, [], [("R", c)] + bk(k))
+            ts(T.R[:, a:b], part(k, 0, b - a), 0.0, None, A.max, None, [], keys_)
         else:
-            act(o, BANK[k], F.Relu, [], [("R", c)] + bk(k))
+            act(T.R[:, a:b], part(k, 0, b - a), F.Relu, [], keys_)
 
     def edges_first():
-        cs = [4 * q + y for q in order for y in range(4)]
+        cs = [(2048 * q + 512 * y, 512) for q in order for y in range(4)]
+        cs[14:] = [(c + x, 256) for c, m in cs[14:] for x in (0, 256)]
+        last = len(cs)
 
         def fetch(j):
-            c, k = cs[j], TURN[j % 6]
-            cp("va"[j % 2], T.TT[:, 512 * c:512 * c + 512], T.P[:, 0:8192].indirect(T.PL[:, 32 * c:32 * c + 32]),
-               PK + [("PL", c // 4)], [("TT", c)])
-            mm(BANK[k], T.SW[0:8, c // 4, :], T.W[0:8, 512 * (c % 4):512 * (c % 4) + 512], True, False, WK + [("SW", c // 4)], bk(k))
-            mm(BANK[k], T.C[:], T.TT[:, 512 * c:512 * c + 512], False, True, CK + [("TT", c)], bk(k))
-        for j in range(20):
-            if j < 16:
+            (c, m), k = cs[j], TURN[j % 6]
+            keys_ = [("TT", x) for x in range(c // 256, (c + m) // 256)]
+            cp("va"[j % 2], T.TT[:, c:c + m], T.P[:, 0:8192].indirect(T.PL[:, c // 16:(c + m) // 16]), PK + [("PL", c // 2048)], keys_)
+            mm(part(k, 0, m), T.C[:], T.TT[:, c:c + m], True, False, CK + keys_, bk(k))
+            for a in range(m // 128):
+                mm(part(k, 128 * a, 128 * a + 128), T.SELI[mine, c % 2048 // 128 + a, :], T.Yw[mine, c // 2048, :], False,
+                   a == m // 128 - 1, [("Yw", c // 2048)], bk(k))
+        for j in range(last + 4):
+            if j < last:
                 fetch(j)
-            if j == 12:
+            if j == WHEN[0]:
                 numbers(); lists_mm(0, 7, 0)
-            if j == 13:
+            if j == WHEN[0] + 1:
                 lists_mm(0, 7, 1)
-            if j == 16:
-                lists(0, 7); steps_mm(0, range(4))
+            if j == WHEN[1]:
+                lists(0, 7)
+            if j == last:
+                steps_mm(0, range(4))
             if j >= 4:
-                relu("a" if j == 16 else "va"[j % 2], cs[j - 4], TURN[(j - 4) % 6])
+                c, m = cs[j - 4]
+                relu("a" if j == WHEN[2] else "va"[j % 2], c, c + m, TURN[(j - 4) % 6])
         for h in range(2):
-            dma("s", T.TT[16 * h:16 * h + 1, 0:8192], T.W[h:8:2, :], "dt", WK, TK if h == 0 else ["TTb"])
+            dma("s", T.TT[16 * h + 15:16 * h + 16, 0:8192], T.W[h:8:2, :], "dt", WK, TK if h == 0 else ["TTb"])
 
     def edges_again():
-        for c in range(16):
-            mm(BANK[TURN[c % 6]], T.C2[:], T.TT[:, 512 * c:512 * c + 512], True, True, ["C2"] + TK, bk(TURN[c % 6]))
-            relu("va"[c % 2], c, TURN[c % 6])
+        cuts = [0, 256, 512, 768] + list(range(1024, 8193, 512))
+        for j in range(len(cuts) - 1):
+            a, b, k = cuts[j], cuts[j + 1], TURN[j % 6]
+            mm(part(k, 0, b - a), T.C2[:], T.TT[:, a:b], True, True, ["C2"] + TK, bk(k))
+            relu("av"[j % 2], a, b, k)
 
     def spread(y):
-        k = (3, 6)[y % 2]
+        k = (3, 1)[y % 2]
+        buf = (T.E1, T.KS)[y % 2]
         for a in range(4 * y, 4 * y + 4):
-            c0 = 128 * (a % 4)
-            mm(part(k, c0, c0 + 128), T.SELI[0:96, a, :], T.DT[0:96, :], True, True, [("SELI", a), "DT", "DT1"], bk(k))
-        sign("a", T.P2[:, 512 * y:512 * y + 512], k, [("P2", y)])
+            c0 = 512 * (y % 2) + 128 * (a % 4)
+            for x in range(2):
+                mm(buf[64 * x:64 * x + 64, c0:c0 + 128], T.SELI[32 * x:32 * x + 32, a, 0:64], T.DT[32 * x:32 * x + 32, :], True, True,
+                   [("SELI", a), "DT"], bk(k))
 
-    CUT = [32, 32, 24, 24]
+    def spread_out(y):
+        ramp("a", T.P2[:, 512 * y:512 * y + 512], (3, 1)[y % 2], [("P2", y)])
+
     for t in range(3):
         pi = t % 2
         if t == 0:
@@ -465,10 +459,10 @@ def rank_program(g, core, T, topo):
                 if term == 1:
                     mm(o, T.G[:, 1024 * q + c:1024 * q + 1024:8], T.R1[:], False, c == 7, [("G", q, "v"), ("G", q, "a"), "R1"], bk(q))
                 elif t < 2:
-                    mm(o, T.P[:, 2048 * q + 2 * c + pi:2048 * q + 2048:16], T.R2[:], False, False, PK + R2K, bk(q))
+                    mm(o, T.P[0:64, 2048 * q + 2 * c + pi:2048 * q + 2048:16], T.R2[0:64, :], False, False, PK + R2K, bk(q))
                 else:
-                    a = 8 * q + c
-                    mm(o, T.P2[:, 128 * a:128 * a + 128], T.R2[:], False, False, [("P2", a // 4)] + R2K, bk(q))
+                    a, x = 8 * (q % 2) + c, slice(64 * (q // 2), 64 * (q // 2) + 64)
+                    mm(o, T.P2[x, 128 * a:128 * a + 128], T.R2[x, :], False, False, [("P2", a // 4)] + R2K, bk(q))
 
         def best(q):
             scan(T.SC[:, 256 * q:256 * q + 256], T.MSK[:], BANK[q][:, 0:256], A.add, A.min, ["MSK"], [("SC", q)] + bk(q))
@@ -477,7 +471,7 @@ def rank_program(g, core, T, topo):
             if t == 0 and j < 2:
                 lists_mm(1, 6, j)
             if t == 1:
-                steps_mm(1, [j] if j < 2 else [2, 3])
+                steps_again(1, [j] if j < 2 else [2, 3])
 
         keys(0, 0); keys(1, 0)
         fetch(0); keys(0, 1); keys(2, 0); aside(0)
@@ -488,11 +482,25 @@ def rank_program(g, core, T, topo):
         if t == 0:
             lists(1, 6)
             act(T.NID[:], T.IDN[:], F.Identity, ["IDN"], ["NID"], scale=-1.0)
-        X = T.E4[:, 0:16, 0:9]
-        mm(X, T.ONE[0:1, :], T.ZR[0:1, 0:144], True, False, ["ONE", "ZR"], bk(6))
+            for x in range(2):
+                for q in range(4):
+                    dma("s", T.WL[32 * q:32 * q + 32, x, :], T.IL[0:32, x, 64 * q:64 * q + 64], "wl", [("IL", x)], [("WL", x, q)])
+        X = T.E4[:, 0:24, 0:9]
+        mm(X, T.ONE[0:1, :], T.ZR[0:1, 0:216], True, False, ["ONE", "ZR"], bk(6))
         best(3)
-        if t < 2:
-            steps_high(pi)
+        if t == 0:
+            steps_high(pi); steps_again(pi, range(4))
+        else:
+            if t == 1:
+                spread(1); spread(0)
+            cp("a", T.GW[:], T.WT[:].indirect(T.WL[:, pi, :]), WTK + ["WTb", "WTc"] + [("WL", pi, q) for q in range(4)], ["GW"])
+            for c in range(8):
+                mm(T.KS[:, c:64:8], T.GW[:, c::8], T.SW[:], True, True, ["GW", "SW"], bk(0))
+            if t == 1:
+                steps_low(pi)
+            cp("a", T.WV[:], T.KS[:, 0:64], [], ["WV"] + bk(0))
+            mm(T.E4[:, 16:24, 1:9], T.BD[:], T.WV[:], False, False, ["BD", "WV"], bk(6))
+            mm(T.E4[:, 16:24, 0:8], T.NBD[:], T.WV[:], False, False, ["NBD", "WV"], bk(6))
 
         SCK = [("SC", q) for q in range(4)]
         key = T.SC[:, 15::16]
@@ -512,15 +520,17 @@ def rank_program(g, core, T, topo):
             mm(T.E4[:, 8 + 4 * h:12 + 4 * h, 1:9], T.BD[:], T.BB[:, h::2], False, False, ["BD", "BB"], bk(6))
             mm(T.E4[:, 8 + 4 * h:12 + 4 * h, 0:8], T.NBD[:], T.BB[:, h::2], False, False, ["NBD", "BB"], bk(6))
         mm(T.E4[:, 0:8, 1:9], T.BD[:], T.TL[:], False, True, ["BD", ("TL", 0), ("TL", 1)], bk(6))
-        if t < 2:
+        if t == 0:
             steps_low(pi)
-        cp("a", T.M1[:, pi, 0:2], X, [], [("M1d", pi)] + bk(6))
+        cp("a", T.M1[:, pi, 0:3], X, [], [("M1d", pi)] + bk(6))
         for u in range(8):
             ts(T.U[:, u, :], T.IOTA[:], T.E0[:, u:u + 1], None, A.is_ge, None, ["IOTA"], [("U", u)] + bk(2))
-        for u in range(8):
-            mm(T.PM[:, 2:6, 9 * u:9 * u + 9], T.U[:, u, :], T.M2[:, pi, :, u, :], False, False, [("U", u), ("M2", pi, u % 4)], bk(7))
-            mm(T.PM[:, :, 9 * u:9 * u + 9], T.U[:, u, :], T.M1[:, pi, :, u, :], False, u == 7,
-               [("U", u), ("M1", pi, u % 4), ("M1d", pi)], bk(7))
+        for us in (range(6), range(6, 8)):
+            for u in us:
+                mm(T.PM[:, 3:7, 9 * u:9 * u + 9], T.U[:, u, :], T.M2[:, pi, :, u, :], False, False, [("U", u), ("M2", pi, u % 4)], bk(7))
+            for u in us:
+                mm(T.PM[:, :, 9 * u:9 * u + 9], T.U[:, u, :], T.M1[:, pi, :, u, :], False, u == 7,
+                   [("U", u), ("M1", pi, u % 4), ("M1d", pi)], bk(7))
         mm(T.E2[:, 0:64], T.IDN[:], T.LL[:], True, False, ["IDN"] + LK, bk(4))
         for h in range(2):
             mm(T.E2[:, 32 * h:32 * h + 32], T.D512[:], T.FF[:, h::2], False, False, ["D512", "FF"], bk(4))
@@ -530,45 +540,60 @@ def rank_program(g, core, T, topo):
             tt(T.OWN[:, 32 * h:32 * h + 32], T.ZZ[:, h::2], T.BB[:, h::2], A.subtract, ["ZZ", "BB"], [("OWN", h)])
             act(T.BST[:, 32 * h:32 * h + 32], T.BB[:, h::2], F.Identity, ["BB"], [("BST", h)], scale=1.0 / 32, bias=31.0)
         OK = [("OWN", 0), ("OWN", 1)]
-        ts(T.NS[:], T.PM[:, 0, :], col(16), None, A.not_equal, None, ["c16"], ["NS"] + bk(7))
+        if t == 1:
+            spread_out(1); spread_out(0)
+        ts(T.NS[:], T.PM[:, 0, :], NEXT, None, A.not_equal, None, ["NEXT"], ["NS"] + bk(7))
         tt(T.DL[:], T.BST[:], T.OWN[:], A.subtract, [("BST", 0), ("BST", 1)] + OK, ["DL"])
         scan(T.SB[:, 9:81], T.NS[:], T.PM[:, 1, :], A.mult, A.add, ["NS"], ["SB"] + bk(7))
-        mm(T.E0[0:9, 0:128], T.SB[:, 8:81:9], T.PERM[:], True, True, ["SB", "SB0", "PERM"], bk(2))
-        cp("a", T.BT[0:9, :], T.E0[0:9, 0:128], [], ["BT"] + bk(2))
+        if t > 0:
+            scan(T.SB[:, 81:153], T.NS[:], T.PM[:, 2, :], A.mult, A.add, ["NS"], ["SBw"] + bk(7))
+        mm(T.E0[0:17, 0:128], T.SB[:, 8:153:9], T.PERM[:], True, True, ["SB", "SBw", "PERM"], bk(2))
+        cp("a", T.BT[0:17, :], T.E0[0:17, 0:128], [], ["BT"] + bk(2))
         for q in range(4):
-            mm(T.E4[:, :, 4 * q:4 * q + 4], T.SELD[0:9, q, :], T.BT[0:9, :], True, True, [("SELD", q), "BT"], bk(6))
-        sign("a", T.DS[:], 6, ["DS"])
+            mm(T.E4[:, :, 4 * q:4 * q + 4], T.SELD[0:17, q, :], T.BT[0:17, :], True, True, [("SELD", q), "BT"], bk(6))
+        ramp("a", T.DS[:], 6, ["DS"])
         for i in range(4):
-            scan(T.SI[:, 72 * i:72 * i + 72], T.NS[:], T.PM[:, 2 + i, :], A.mult, A.add, ["NS"], [("SI", i)] + bk(7))
+            scan(T.SI[:, 72 * i:72 * i + 72], T.NS[:], T.PM[:, 3 + i, :], A.mult, A.add, ["NS"], [("SI", i)] + bk(7))
         ts(T.GO[:], T.E2[:, 0:64], -383.5, None, A.is_lt, None, [], ["GO"] + bk(4))
-        for z in range(4):
-            ts(T.ST[:, z::4], T.SI[:, 8::9], T.MZ[:, z:z + 1], None, A.mult, None, [("SI", i) for i in range(4)] + ["MZ"], [("ST", z)])
-        mm(T.E1[:, 0:32], T.ST[:], T.EI[:], True, True, [("ST", z) for z in range(4)] + ["EI"], bk(3))
+        for x in range(4):
+            scaled("v", T.ST[:, x::4], T.SI[:, 8::9], T.MZ[:, x:x + 1], [("SI", i) for i in range(4)] + ["MZ"], [("ST", x)])
+        mm(T.E1[:, 0:32], T.ST[:], T.EI[:], True, True, [("ST", x) for x in range(4)] + ["EI"], bk(3))
         tt(T.GD[:], T.GO[:], T.DL[:], A.mult, ["GO", "DL"], ["GD"])
         cp("v", T.OFF[:], T.E1[:, 0:32], [], ["OFF"] + bk(3))
-        if t == 0:
-            mm(T.E2[0:64, 0:128], T.OWN[:], T.IDN[:], True, False, OK + ["IDN"], bk(4))
-            mm(T.E2[0:64, 0:128], T.GD[:], T.IDN[:], False, True, ["GD", "IDN"], bk(4))
-            cp("a", T.DT[0:64, :], T.E2[0:64, 0:128], [], ["DT"] + bk(4))
-            mm(BANK[1][:, 0:128], T.DNZ[:], T.C[:], True, False, ["DNZ"] + CK, bk(1))
-            mm(BANK[1][:, 0:128], T.RS[0:4, :], T.SP[0:4], False, True, ["RS", "SP"], bk(1))
-            cp("a", T.C2[:], BANK[1][:, 0:128], [], ["C2"] + bk(1))
-        else:
-            mm(T.E2[:, 0:64], T.IDN[:], T.OWN[:], True, False, OK + ["IDN"], bk(4))
-            mm(T.E2[:, 0:64], T.IDN[:], T.GD[:], False, True, ["GD", "IDN"], bk(4))
-            for h in range(2):
+        mm(T.E2[:, 0:64], T.IDN[:], T.OWN[:], True, False, OK + ["IDN"], bk(4))
+        mm(T.E2[:, 0:64], T.IDN[:], T.GD[:], False, True, ["GD", "IDN"], bk(4))
+        for h in range(2):
+            if t == 0:
+                cp("a", T.NB[:, :, h, :], T.E2[:, 32 * h:32 * h + 32], [], [("NB", h)] + bk(4))
+            else:
                 cp("a", T.NPO[:, :, h, pi::2], T.E2[:, 32 * h:32 * h + 32], [], [("NPO", pi, h)] + bk(4))
-        tt(T.DG[:], T.WT[:].indirect(T.OFF[:]), T.DS[:], A.mult, WTK + ["WTb", "OFF", "DS"], ["DG"])
-        cp("v", T.TT[:].indirect(T.OFF[:]), T.DG[:], ["DG", "OFF"], TK + ["TTb"])
-        if t < 2:
-            for y in range(4 * t, 4 * t + 4):
-                spread(y)
+        if t == 0:
+            steps_mm(1, range(4))
+            mm(BANK[1][:, 0:128], T.DNZ[:], T.C[:], True, False, ["DNZ"] + CK, bk(1))
+            for s_ in range(2):
+                mm(BANK[1][:, 0:128], T.RS[0:4, s_, :], T.SP[0:4, s_], False, s_ == 1, [("RS", s_), ("SP", s_)], bk(1))
+            mm(T.E0[0:64, 0:128], T.NB[:], T.IDN[:], True, True, [("NB", 0), ("NB", 1), "IDN"], bk(2))
+            cp("a", T.C2[:], BANK[1][:, 0:128], [], ["C2"] + bk(1))
+            cp("a", T.DT[0:64, :], T.E0[0:64, 0:128], [], ["DT"] + bk(2))
+        if t == 0:
+            tt(T.DG[:], T.WT[:].indirect(T.OFF[:]), T.DS[:], A.mult, WTK + ["WTb", "OFF", "DS"], ["DG"])
+            cp("v", T.TT[:].indirect(T.OFF[:]), T.DG[:], ["DG", "OFF"], TK + ["TTb"])
+            for x in range(2, 8):
+                dma("s", T.WT[16 * x + 15:16 * x + 16, 0:8192], T.W[x % 2:8:2, :], "w4", WK, WTK if x == 2 else ["WTc"] if x == 7 else [])
+            steps_high(1)
         else:
+            cp("v", T.TT[:].indirect(T.OFF[:]), T.DS[:], ["DS", "OFF"], TK)
+        if t == 1:
+            spread(3); spread(2); spread_out(3); spread_out(2)
+        if t == 2:
             mm(BANK[1][:, 0:32], T.DNZ[:], T.Z[:], True, False, ["DNZ", "Z"], bk(1))
-            mm(BANK[1][:, 0:32], T.RS[0:4, :], T.SQ[0:4], False, True, ["RS", "SQ"], bk(1))
+            for s_ in range(2):
+                mm(BANK[1][:, 0:32], T.RS[0:4, s_, :], T.SP[0:4, s_, 2:4], False, s_ == 1, [("RS", s_), ("SP", s_)], bk(1))
             for h in range(2):
                 cp("a", T.CC[:, :, h], BANK[1][:, 16 * h:16 * h + 16], [], [("CC", h)] + bk(1))
-            act(T.Yj[64:128], T.Yw[64:128], F.Identity, [("Yw", q) for q in range(4)], ["Yj", ("ACC", 8)], accum_out=T.ACC[64:128, 8:9])
+            act(T.Yj[mine], T.Yw[mine], F.Identity, [("Yw", q) for q in range(4)], ["Yj", ("ACC", 10)],
+                accum_out=T.ACC[mine, 10:11])
+            scaled("a", T.MW[:], T.HM[:, 0:32:16], 15.0, ["HM"], ["MW"])
 
     NK = [("NPO", pi, h) for pi in range(2) for h in range(2)]
     fused(1, "oa", lambda b: T.NPO[:, b], T.LO[:, me], NK)
@@ -578,28 +603,28 @@ def rank_program(g, core, T, topo):
             dma("s", T.newpart[2 * b + h:2 * b + h + 1, :], src, "dn", keys_, [])
 
     cutp = T.E3[0:1, 0:2]
-    mm(cutp, T.ACC[64:128, 8:9], T.MW[64:128, :], True, False, [("ACC", 8), "MW"], bk(5))
-    for k in range(4):
-        for a in range(16):
-            c0 = 2048 * k + 128 * a
+    mm(cutp, T.ACC[mine, 10:11], T.MW[mine, :], True, False, [("ACC", 10), "MW"], bk(5))
+    a0 = 0
+    for k, (m, who) in enumerate(PIECES):
+        for a in range(m):
+            c0 = 128 * (a0 + a)
             mm(BANK[k][:, 32 * a:32 * a + 32], T.TT[:, c0:c0 + 128], T.CC[:], True, True, TK + [("CC", 0), ("CC", 1)], bk(k))
+        a0 += m
         for h in range(2):
             j = 2 * k + h
-            junk = T.R[:, 512 * j:512 * j + 256]
-            if k == 1:
-                ts(junk, BANK[k][:, h::2], 0.0, None, A.max, None, [], [("R", j)] + bk(k))
+            junk = T.R[:, 512 * j:512 * j + 16 * m]
+            if who[h] == "v":
+                ts(junk, BANK[k][:, h:32 * m:2], 0.0, None, A.max, None, [], [("R", j)] + bk(k))
             else:
-                act(junk, BANK[k][:, h::2], F.Relu, [], [("R", j), ("ACC", j)] + bk(k), accum_out=T.ACC[:, j:j + 1])
-    for j in (2, 3):
-        op("v", lambda: V.tensor_reduce(T.ACC[:, j:j + 1], T.R[:, 512 * j:512 * j + 256], AX.X, A.add), [("R", j)], [("ACC", j)])
-    for k in range(4):
-        mm(cutp, T.NG[:], T.ACC[:, 2 * k:2 * k + 2], False, k == 3, [("ACC", 2 * k), ("ACC", 2 * k + 1), "NG"], bk(5))
+                act(junk, BANK[k][:, h:32 * m:2], F.Relu, [], [("R", j), ("ACC", j)] + bk(k), accum_out=T.ACC[:, j:j + 1])
+        for h in range(2):
+            j = 2 * k + h
+            if who[h] == "v":
+                op("v", lambda: V.tensor_reduce(T.ACC[:, j:j + 1], T.R[:, 512 * j:512 * j + 16 * m], AX.X, A.add), [("R", j)], [("ACC", j)])
+    for k in range(len(PIECES)):
+        mm(cutp, T.NG[:], T.ACC[:, 2 * k:2 * k + 2], False, k == len(PIECES) - 1, [("ACC", 2 * k), ("ACC", 2 * k + 1), "NG"], bk(5))
     cp("v", T.CL[0:1, me, 0:2], cutp, [], ["CLown"] + bk(5))
-    deps("g", ["CLown"], [])
-    en = [e for x in share(me, 0).values() for e in x]
-    g.remote_dma_fused([RemoteDMATransfer(dst_ids=[dst(b) for b in others], dma_engine_mask=bits(en), remote_sem=T.sem.ca,
-                                          srcs=[T.CL[:, me, :]], dsts=[T.CL[:, me, :] for b in others])], local_sem=T.sem.sent)
-    cnt["sent"] += len(en)
+    to_all(T.sem.ca, T.CL[:, me, :], ["CLown"])
     dma("a", T.cut[:], T.CL[0:1, :, 0:2], "dc", ["CLown", "CLfar"], [])
 
     for s in SEMAPHORES:

from concourse.bass import DstId, RemoteDMATransfer
from concourse.mybir import AluOpType as A, ActivationFunctionType as F, AxisListType as AX

R2048, R128, R32 = 1.5 * 2.0 ** 34, 1.5 * 2.0 ** 30, 1.5 * 2.0 ** 28
WIN = 8192 + 512
SEED = WIN // 16
CUT = [32, 30, 30, 30]
WHEN = [12, 18, 18]
PIECES = [(12, "aa"), (12, "vv"), (16, "aa"), (10, "vv"), (14, "aa")]
SCRATCH = {
    "DI": ("dram", [4, 128, 128], "int32"),
    "KS": ("psum", [128, 1024], "float32"),
    "E0": ("psum", [128, 512], "float32"),
    "E1": ("psum", [128, 512], "float32"),
    "E2": ("psum", [128, 512], "float32"),
    "E3": ("psum", [128, 512], "float32"),
    "E4": ("psum", [128, 32, 16], "float32"),
    "PM": ("psum", [128, 7, 72], "float32"),
}
for _names, _shape, _dt in [
        ("YI", [256], "int32"), ("Y Yw Yj", [4, 128], "bfloat16"), ("W", [2048], "bfloat16"),
        ("S32 NL", [4, 128], "int32"), ("S16 PL", [512], "uint16"), ("IL", [2, 256], "uint16"),
        ("OFF", [32], "uint16"), ("P R", [8192], "bfloat16"), ("TT WT", [WIN], "bfloat16"), ("G", [4096], "bfloat16"), ("P2", [2048], "bfloat16"),
        ("MX", [4, 8, 2, 8], "float32"), ("KI", [4], "int32"), ("CI", [4], "int32"), ("CF", [8], "float32"),
        ("J32 EI", [32], "float32"), ("EJ", [16], "float32"), ("NE MZ", [4], "float32"),
        ("JH HM C C2 ONE IDN NID TRI SH BD NBD D512 PERM IOTA OS BT DT DNZ REP S0", [128], "bfloat16"),
        ("SELI", [16, 128], "bfloat16"), ("SELD", [4, 128], "bfloat16"), ("U", [8, 128], "bfloat16"),
        ("Z0 Z KT R1 R2 MK8", [32], "bfloat16"), ("CC", [16, 2], "bfloat16"), ("SP", [2, 8, 16], "bfloat16"), ("RS", [2, 128], "bfloat16"),
        ("DS DG", [512], "bfloat16"), ("KC", [256], "bfloat16"), ("ZR", [288], "bfloat16"),
        ("MSK", [256], "float32"), ("MW", [2], "float32"), ("NG", [1], "float32"),
        ("SC", [1024], "float32"), ("KR ZZ", [64], "float32"), ("NS", [72], "float32"),
        ("FF LL TL BB OWN BST GO DL GD", [64], "bfloat16"), ("NB", [2, 2, 16], "bfloat16"), ("SB", [160], "bfloat16"),
        ("SI TM", [288], "float32"), ("ST", [128], "float32"), ("X32", [4, 132], "float32"), ("MD", [4, 8, 9], "float32"),
        ("OM", [7, 8, 9], "bfloat16"), ("M1", [2, 7, 8, 9], "bfloat16"), ("WL", [2, 64], "uint16"), ("GW", [1024], "bfloat16"),
        ("SW", [8], "bfloat16"), ("WV", [64], "bfloat16"), ("M2", [2, 4, 8, 9], "bfloat16"),
        ("NPO LO", [4, 2, 16], "float32"), ("ACC", [12], "float32"), ("CL", [4, 4], "float32")]:
    for _n in _names.split():
        SCRATCH[_n] = ("sbuf", [128] + _shape, _dt)
SEMAPHORES = (["ev", "ea", "et", "eg", "dy", "dyw", "dp", "di", "dio", "dw", "dt", "w1", "w2", "w3", "w4", "wl", "dn", "dc", "ca", "sy", "sent"]
              + ["%s%d" % (n, q) for n in ("ya", "wa", "pa", "ia", "oa") for q in range(4)])


def rank_program(g, core, T, topo):
    me = T.rank_of(core)
    if me is None:
        return
    cores = T.cores
    n = len(cores)
    Q = {"v": g.vector, "a": g.scalar, "t": g.tensor, "g": g, "s": g.sync}
    own = {"v": "ev", "a": "ea", "t": "et", "g": "eg"}
    cnt = dict((s, 0) for s in SEMAPHORES)
    clock = dict((q, {}) for q in Q)
    waited = dict((s, 0) for s in SEMAPHORES)
    wr, rd = {}, {}

    def need(q, tok):
        s, v, ck, src = tok
        if src == "t" and q == "t":
            return
        if v is None:
            v = cnt[s]
        if clock[q].get(s, 0) < v:
            Q[q].wait_ge(T.sem[s], v)
            waited[s] = max(waited[s], v)
            clock[q][s] = v
        for k in ck:
            if clock[q].get(k, 0) < ck[k]:
                clock[q][k] = ck[k]

    def deps(q, reads, writes):
        toks = [wr[k] for k in list(reads) + list(writes) if k in wr and not (k[:1] == ("B",) and wr[k][3] == q)]
        for k in writes:
            toks += rd.get(k, [])
        toks.sort(key=lambda t: -(t[1] if t[1] is not None else cnt[t[0]]))
        for t in toks:
            need(q, t)

    def mark(tok, reads, writes):
        for k in writes:
            wr[k] = tok
            rd[k] = []
        for k in reads:
            rd.setdefault(k, []).append(tok)

    def op(q, call, reads, writes):
        deps(q, reads, writes)
        s = own[q]
        cnt[s] += 1
        call().then_inc(T.sem[s], 1)
        mark((s, cnt[s], dict(clock[q]), q), reads, writes)

    def dma(q, out, in_, s, reads, writes):
        deps(q, reads, writes)
        cnt[s] += 16
        Q[q].dma_start(out, in_).then_inc(T.sem[s], 16)
        mark((s, None, dict(clock[q]), "dma"), reads, writes)

    def lands(key, s, v):
        cnt[s] += v
        wr[key] = (s, None, {}, "far")

    V, S, PE = g.vector, g.scalar, g.tensor

    def ts(out, in0, s1, s2, o0, o1, reads, writes):
        if o1 is None:
            op("v", lambda: V.tensor_scalar(out, in0, s1, None, o0), reads, writes)
        else:
            op("v", lambda: V.tensor_scalar(out, in0, s1, s2, o0, o1), reads, writes)

    def tt(out, a, b, o, reads, writes):
        op("v", lambda: V.tensor_tensor(out, a, b, o), reads, writes)

    def scan(out, a, b, o0, o1, reads, writes):
        op("v", lambda: V.tensor_tensor_scan(out, a, b, 0.0, o0, o1), reads, writes)

    def act(out, in_, f, reads, writes, **kw):
        op("a", lambda: S.activation(out, in_, f, **kw), reads, writes)

    def cp(q, out, in_, reads, writes):
        if q == "v":
            op("v", lambda: V.tensor_copy(out, in_), reads, writes)
        else:
            act(out, in_, F.Copy, reads, writes)

    def scaled(e, out, in_, c, reads, writes):
        if e == "a":
            act(out, in_, F.Identity, reads, writes, scale=c)
        else:
            ts(out, in_, c, None, A.mult, None, reads, writes)

    def mm(out, l, r, st, sp, reads, writes):
        op("t", lambda: PE.matmul(out, l, r, st, sp), reads, writes)

    def io(out, pat, base, cm, writes, flag=True):
        if flag:
            op("g", lambda: g.iota(out, pat, base, cm, allow_small_or_imprecise_dtypes=True), ["POOL"], writes)
        else:
            op("g", lambda: g.iota(out, pat, base, cm), ["POOL"], writes)

    def af(out, in_, pat, cmp, fill, base, cm, reads, writes):
        op("g", lambda: g.affine_select(out, in_, pat, cmp, fill, base, cm), reads + ["POOL"], writes)

    def put_in(ap, pat, fill, base, key):
        af(ap, ap, pat, A.not_equal, fill, base, 1, [], [key])

    def hops(a, b):
        ca, cb = topo.chip(cores[a]), topo.chip(cores[b])
        return 0 if ca == cb else 1 if topo.mates(ca, cb) else 2 if topo.same_plane(ca, cb) else 3

    def peers(a):
        return sorted([b for b in range(n) if b != a], key=lambda b: (hops(a, b), b))

    def engines(a):
        ps = peers(a)
        return [e for e in topo.engines(cores[a], cores[ps[0]]) if all(e in topo.engines(cores[a], cores[b]) for b in ps)]

    def share(a, turn):
        en = engines(a)
        k = len(en) // 4
        cuts = [en[:2 * k], en[2 * k:3 * k], en[3 * k:4 * k]]
        return dict((b, cuts[(j + turn) % 3]) for j, b in enumerate(peers(a)))

    def bits(en):
        return sum(1 << e for e in en)

    def dst(b):
        rid, pid, _e = topo.addr(cores[b])
        return DstId(rid=rid, pnc=pid)

    def fused(turn, name, src, land, reads):
        deps("g", reads, [])
        sh = share(me, turn)
        g.remote_dma_fused([RemoteDMATransfer(dst_ids=[dst(b)], dma_engine_mask=bits(sh[b]),
                                              remote_sem=T.sem["%s%d" % (name, me)], src=src(b), dst=land)
                            for b in others], local_sem=T.sem.sent)
        cnt["sent"] += sum(len(sh[b]) for b in others)

    def to_all(sem, ap, reads, left="sent"):
        deps("g", reads, [])
        g.remote_dma_fused([RemoteDMATransfer(dst_ids=[dst(b) for b in others], dma_engine_mask=bits(engines(me)), remote_sem=sem,
                                              srcs=[ap], dsts=[ap for b in others])], local_sem=T.sem[left])
        lands(left, left, len(engines(me)))

    others = peers(me)
    order = [me] + others
    for b in others:
        lands(("Y", b), "ya%d" % b, len(engines(b)))
        lands(("Yw", b), "wa%d" % b, len(engines(b)))
        lands(("PL", b), "pa%d" % b, len(share(b, 0)[me]))
        lands(("NL", b), "ia%d" % b, len(share(b, 1)[me]))
        lands(("LO", b), "oa%d" % b, len(share(b, 1)[me]))
        lands("CLfar", "ca", len(engines(b)))

    dma("s", T.YI[:, 0:128], T.part[:], "dy", [], [("YI", 0)])
    dma("s", T.YI[:, 128:256], T.w[:], "dyw", [], [("YI", 1)])
    for r in range(4):
        for i in range(4):
            dma("sa"[i // 2], T.S32[32 * i:32 * i + 32, r, :], T.pin[32 * r:32 * r + 32, 128 * i:128 * i + 128], "dp", [], [("S32", r, i)])
    S32K = [("S32", r, i) for r in range(4) for i in range(4)]
    dma("s", T.DI[:], T.inc[:], "di", [], ["DI"])
    mine = slice(32 * me, 32 * me + 32)

    io(T.KI[:, 0:1], [[0, 1]], 0, 1, ["KI"], False)
    io(T.J32[:], [[1, 32]], 0, 0, ["J32"])
    io(T.JH[:], [[0, 4], [1, 2], [0, 16]], 0, 0, ["JH"])
    io(T.Z0[0:32, :], [[0, 32]], 0, 0, ["Z0"])
    io(T.ONE[:], [[0, 128]], 1, 0, ["ONE"])
    z = T.Z0[0:32, :]
    put_in(z, [[-1, 32]], -16.0, -1, "Z0")
    af(T.REP[0:32, :], T.ONE[0:32, :], [[0, 4], [-1, 32]], A.is_equal, 0.0, 0, 1, ["ONE"], ["REP"])
    put_in(z, [[-1, 32]], -16.0, 1, "Z0")
    put_in(z, [[-1, 32]], 32.0, 0, "Z0")

    for j, (sh_, an) in enumerate([(0, 15), (4, 1), (0, 31), (5, 3)]):
        ts(T.CI[:, j:j + 1], T.KI[:, 0:1], sh_, an, A.logical_shift_right, A.bitwise_and, ["KI"], [("CI", j)])
    cp("v", T.CF[:, 0:4], T.CI[:], [("CI", j) for j in range(4)], ["CF"])

    def col(j):
        return T.CF[:, j:j + 1]
    ts(T.EJ[:], T.J32[:, 0:16], col(0), None, A.is_equal, None, ["J32", "CF"], ["EJ"])
    ts(T.HM[:], T.JH[:], col(1), None, A.is_equal, None, ["JH", "CF"], ["HM"])
    BIAS = col(4)
    ts(BIAS, T.EJ[:, 15:16], 16.0, col(0), A.mult, A.subtract, ["EJ", "CF"], ["BIAS"])
    for a in range(16):
        scaled("va"[a % 2], T.SELI[:, a, :], T.HM[:], T.EJ[:, a:a + 1], ["HM", "EJ"], [("SELI", a)])
        if a == 10:
            cp("v", T.Y[:, me, :], T.YI[:, 0:128], [("YI", 0)], [("Y", me)])
            cp("v", T.Yw[:, me, :], T.YI[:, 128:256], [("YI", 1)], [("Yw", me)])
    to_all(T.sem["ya%d" % me], T.Y[:, me, :], [("Y", me)])
    to_all(T.sem["wa%d" % me], T.Yw[:, me, :], [("Yw", me)])
    ts(T.EI[:], T.J32[:], col(2), None, A.is_equal, None, ["J32", "CF"], ["EI"])
    ts(T.MZ[:], T.J32[:, 0:4], col(3), None, A.is_equal, None, ["J32", "CF"], ["MZ"])

    BANK = [T.KS[:, 0:512], T.KS[:, 512:1024], T.E0[:], T.E1[:], T.E2[:], T.E3[:], T.E4[:]]
    TURN = [0, 1, 2, 3, 4, 6]

    def bk(k):
        return [("B", k)]

    def part(k, a, b):
        return T.E4[:, a // 16:b // 16, :] if k == 6 else T.PM[:, a // 64:b // 64, 0:64] if k == 7 else BANK[k][:, a:b]

    def ramp(e, out, k, writes):
        if e == "v":
            ts(out, BANK[k], BIAS, 0.0, A.add, A.max, ["BIAS"], writes + bk(k))
        else:
            act(out, BANK[k], F.Relu, ["BIAS"], writes + bk(k), bias=BIAS)

    PK = [("P", c) for c in range(16)]
    RK = [("R", c) for c in range(32)]
    TK = [("TT", c) for c in range(32)]
    CK = [("C", i) for i in range(4)]

    def take(j):
        q = order[j]
        for y in range(4):
            k = (4 * j + y) % 7
            for a in range(4 * y, 4 * y + 4):
                c0 = 128 * (a % 4)
                mm(part(k, c0, c0 + 128), T.SELI[mine, a, :], T.Y[mine, q, :], True, True, [("SELI", a), ("Y", q)], bk(k))
            ramp("av"[y % 2], T.P[:, 2048 * q + 512 * y:2048 * q + 512 * y + 512], k, [("P", 4 * q + y)])

    take(0)
    cp("v", T.S16[:], T.S32[:], S32K, ["S16"])
    af(z, z, [[-16, 2], [0, 16]], A.is_ge, 0.0, 0, 1, [], ["Z0"])
    io(T.KT[:], [[0, 2], [2, 16]], 66, 0, ["KT"])
    af(z, z, [[16, 2], [0, 16]], A.is_ge, 0.0, 14, -1, [], ["Z0"])
    put_in(T.Z0[0:32, 0::16], [[-16, 2]], -16.0, -15, "Z0")
    fused(0, "pa", lambda b: T.S16[:, 128 * b:128 * b + 128], T.PL[:, 128 * me:128 * me + 128], ["S16"])
    fused(1, "ia", lambda b: T.DI[b], T.NL[:, me], ["DI"])
    cp("v", T.PL[:, 128 * me:128 * me + 128], T.S16[:, 128 * me:128 * me + 128], ["S16"], [("PL", me)])
    act(T.NE[:], T.MZ[:], F.Identity, ["MZ"], ["NE"], scale=-1.0, bias=1.0)
    scaled("a", T.R1[:], T.EI[:], 2048.0, ["EI"], ["R1"])
    mm(T.PM[:, 0, 0:32], T.REP[0:32, :], z, True, True, ["REP", "Z0"], bk(7))
    cp("v", T.Z[:], T.PM[:, 0, 0:32], [], ["Z"] + bk(7))
    tt(T.R2[:], T.PM[:, 0, 0:32], T.KT[:], A.mult, ["KT"], ["R2"] + bk(7))
    for i in range(4):
        scaled("av"[i % 2], T.C[:, 32 * i:32 * i + 32], T.Z[:], T.NE[:, i:i + 1], ["NE", "Z"], [("C", i)])
    take(1); take(2); take(3)
    dma("s", T.NL[:, me, :], T.inc[mine, :], "dio", [("Y", others[0])], [("NL", me)])
    NLK = [("NL", q) for q in range(4)]
    for q in order:
        for h in range(2):
            dma("s", T.W[2 * q + h:2 * q + h + 1, :], T.Yw[32 * me + 16 * h:32 * me + 16 * h + 16, q, :], "dw", [("Yw", q)], [("W", q, h)])
    WK = [("W", q, h) for q in range(4) for h in range(2)]

    def diag(out, base, fill, key, src=None):
        if src is None:
            af(out, T.ONE[:], [[-1, 128]], A.is_equal, 0.0, base, 1, ["ONE"], [key])
        else:
            af(out, T[src][:], [[-1, 128]], A.not_equal, fill, base, 1, [src], [key])
    io(T.MX[:], [[0, 512]], 0, 0, [("MX", j) for j in range(4)])
    io(T.MD[:, 0:2], [[0, 144]], 0, 0, [("MD", 0), ("MD", 1)])
    io(T.WT[:, 0:SEED], [[0, SEED]], 1, 0, [("WT", 0)])
    row = [[-1, 4], [-64, 2], [-8, 8]]
    for j in range(4):
        put_in(T.MX[:, j, :, j % 2, :], row, 1.0, -4 * (j // 2), ("MX", j))
    for x in range(2):
        for pi in range(2):
            put_in(T.MD[:, pi, :, 1 - x:9 - x], row, 1.0 - 2 * x, -4 * pi, ("MD", pi))
    io(T.X32[:, :, 0], [[0, 4]], 0, 0, ["X0"])
    io(T.ZR[0:1, :], [[0, 288]], 0, 0, ["ZR"])
    io(T.KC[0:1, :], [[0, 16], [32, 16]], 1056, 0, ["KC"])
    for x in (32, 96):
        af(T.R2[x:x + 32, :], T.ONE[x:x + 32, 0:32], [[-16, 2], [0, 16]], A.is_equal, 0.0, 0, 1, ["ONE"], ["R2", "POOL"])
    R2K = ["R2"]
    io(T.MSK[:], [[0, 256]], 0, 0, ["MSK"])
    diag(T.IDN[:], 0, None, "IDN")
    io(T.MSK[:, 0::16], [[0, 16]], 262144, 0, ["MSK"])
    io(T.OM[0:2], [[0, 504]], 0, 0, ["OM"])
    io(T.OS[0:2, :], [[1, 128]], 0, 0, ["OS"])
    io(T.OM[0:2, 3:7, :, 0], [[0, 8], [128, 4]], 8192, 0, ["OM"])
    put_in(T.OS[0:2, :], [[0, 128]], 1.0, -1, "OS")
    put_in(T.OM[0:2, 3:7, :, 0], [[0, 32]], 1.0, 0, "OM")
    af(T.MK8[:], T.ONE[:, 0:32], [[0, 4], [1, 8]], A.not_equal, 0.0, 0, 0, ["ONE"], ["MK8"])
    io(T.OM[0:2, 0, :, 0], [[0, 8]], 1, 0, ["OM"])
    af(T.TRI[:], T.ONE[:], [[1, 128]], A.is_gt, 0.0, 0, -1, ["ONE"], ["TRI"])
    diag(T.SH[:], 1, None, "SH")
    io(T.IOTA[:], [[1, 128]], 0, 0, ["IOTA"])
    diag(T.BD[:], 1, -1.0, "BD", "IDN")
    diag(T.NBD[:], 0, -1.0, "NBD", "SH")
    diag(T.D512[:], 0, -512.0, "D512", "IDN")
    NEXT = col(5)
    io(NEXT, [[0, 1]], 1, 1, ["NEXT"])
    io(T.S0[0:17, :], [[0, 128]], 31, 0, ["S0"])
    af(T.PERM[:], T.ONE[:], [[-1, 32], [-32, 4]], A.is_equal, 0.0, 0, 1, ["ONE"], ["PERM"])
    af(T.S0[0:17, :], T.S0[0:17, :], [[0, 128]], A.is_equal, 0.0, 0, 1, [], ["S0"])
    io(T.SB[:, 8:153:9], [[0, 17]], 1, 0, ["SB", "SBw"])
    for q in range(4):
        af(T.SELD[0:17, q, :], T.S0[0:17, :], [[0, 4], [-4, 2], [0, 16]], A.not_equal, 1.0 / 32, -1 - q, 1, ["S0"], [("SELD", q)])
    SELDK = [("SELD", q) for q in range(4)]
    io(T.SELD[0:17, :, 15:32:16], [[0, 8]], 0, 0, SELDK)
    af(T.SW[:], T.ONE[:, 0:8], [[-16, 2], [-32, 4]], A.is_equal, 0.0, -15, 1, ["ONE"], ["SW"])
    for pat, fill, base in (([[-1, 4], [-4, 2]], 1.0, -9), ([[0, 8]], -1.0, 0)):
        af(T.SELD[0:17, :, 15:32:16], T.SELD[0:17, :, 15:32:16], pat, A.not_equal, fill, base, 1, [], SELDK)
    af(T.DNZ[:], T.IDN[:], [[16, 8], [-100, 16]], A.is_gt, 0.0, 1484, 0, ["IDN"], ["DNZ"])
    for s_ in range(2):
        af(T.RS[0:4, s_, :], T.ONE[0:4, :], [[-1, 128]], A.is_equal, 0.0, 15 * s_, 16, ["ONE"], [("RS", s_)])
    io(T.SP[0:4, 0], [[0, 128]], 0, 0, [("SP", 0)])
    af(T.SP[0:4, 1], T.ONE[0:4, :], [[0, 4], [-1, 2], [0, 16]], A.is_equal, 0.0, 0, 1, ["ONE"], [("SP", 1)])
    for s_, fill, base in ((0, -16.0, 0), (1, -16.0, -2), (0, 16.0, -2)):
        put_in(T.SP[0:4, s_, 2:8, 0], [[0, 3], [-1, 2]], fill, base, ("SP", s_))
    io(T.NG[:], [[0, 1]], -1, 0, ["NG"])
    io(T.CL[:, me, :], [[0, 4]], 0, 0, ["CLown"])

    for j in range(1, 4):
        dma("s", T.WT[:, SEED * j:SEED * j + SEED], T.WT[:, 0:SEED], "w1", [("WT", 0)], [("WT", j)])
    for j in range(1, 4):
        dma("s", T.WT[:, 4 * SEED * j:4 * SEED * (j + 1)], T.WT[:, 0:4 * SEED], "w2", [("WT", x) for x in range(4)], [("WT", 3 + j)])
    WTK = [("WT", x) for x in range(7)]
    for h in range(2):
        dma("s", T.WT[16 * h + 15:16 * h + 16, 0:8192], T.W[h:8:2, :], "w3", WK, WTK if h == 0 else ["WTb"])

    def lists_mm(pi, k, x):
        mm(part(k, 0, 256), T.MX[:, 2 * pi + x], T.X32[:, :, 1 + x:129:2], x == 0, x == 1, [("MX", 2 * pi + x), "X32"], bk(k))

    def lists(pi, k):
        cp("v", T.IL[:, pi], part(k, 0, 256), [], [("IL", pi)] + bk(k))

    def numbers():
        cp("v", T.X32[:, :, 1:129], T.NL[:], NLK, ["X32"])
        act(T.MD[:, 2:4], T.MD[:, 0:2], F.Identity, [("MD", 0), ("MD", 1)], ["MDn"], scale=-1.0)

    def steps_mm(pi, qs, close=True):
        for q in qs:
            if q == 0:
                mm(T.E3[:, 0:288], T.ONE[0:1, :], T.ZR[0:1, :], True, False, ["ONE", "ZR"], bk(5))
            o = T.E3[:, 72 * q:72 * q + 72]
            mm(o, T.X32[:, q, 1:129], T.MD[:, pi], False, False, ["X32", ("MD", pi)], bk(5))
            mm(o, T.X32[:, q, 0:128], T.MD[:, 2 + pi], False, close and q == 3, ["X0", "MDn"], bk(5))

    def steps_high(pi):
        act(T.TM[:], T.E3[:, 0:288], F.Identity, [], ["TM"] + bk(5), bias=R128)
        for q in range(4):
            act(T.M1[:, pi, 3:7, q::4, :], T.TM[:, 72 * q:72 * q + 72], F.Identity, ["TM"], [("M1", pi, q)], bias=-R128)

    def steps_again(pi, qs):
        steps_mm(pi, qs, False)
        for q in qs:
            mm(T.E3[:, 72 * q:72 * q + 72], T.NID[:], T.M1[:, pi, 3:7, q::4, :], False, q == 3, ["NID", ("M1", pi, q)], bk(5))

    def steps_low(pi):
        for q in range(4):
            cp("a", T.M2[:, pi, :, q::4, :], T.E3[:, 72 * q:72 * q + 72], [], [("M2", pi, q)] + bk(5))

    def relu(e, a, b, k):
        keys_ = [("R", c) for c in range(a // 256, b // 256)] + bk(k)
        if e == "v":
            ts(T.R[:, a:b], part(k, 0, b - a), 0.0, None, A.max, None, [], keys_)
        else:
            act(T.R[:, a:b], part(k, 0, b - a), F.Relu, [], keys_)

    def edges_first():
        cs = [(2048 * q + 512 * y, 512) for q in order for y in range(4)]
        cs[14:] = [(c + x, 256) for c, m in cs[14:] for x in (0, 256)]
        last = len(cs)

        def fetch(j):
            (c, m), k = cs[j], TURN[j % 6]
            keys_ = [("TT", x) for x in range(c // 256, (c + m) // 256)]
            cp("va"[j % 2], T.TT[:, c:c + m], T.P[:, 0:8192].indirect(T.PL[:, c // 16:(c + m) // 16]), PK + [("PL", c // 2048)], keys_)
            mm(part(k, 0, m), T.C[:], T.TT[:, c:c + m], True, False, CK + keys_, bk(k))
            for a in range(m // 128):
                mm(part(k, 128 * a, 128 * a + 128), T.SELI[mine, c % 2048 // 128 + a, :], T.Yw[mine, c // 2048, :], False,
                   a == m // 128 - 1, [("Yw", c // 2048)], bk(k))
        for j in range(last + 4):
            if j < last:
                fetch(j)
            if j == WHEN[0]:
                numbers(); lists_mm(0, 7, 0)
            if j == WHEN[0] + 1:
                lists_mm(0, 7, 1)
            if j == WHEN[1]:
                lists(0, 7)
            if j == last:
                steps_mm(0, range(4))
            if j >= 4:
                c, m = cs[j - 4]
                relu("a" if j == WHEN[2] else "va"[j % 2], c, c + m, TURN[(j - 4) % 6])
        for h in range(2):
            dma("s", T.TT[16 * h + 15:16 * h + 16, 0:8192], T.W[h:8:2, :], "dt", WK, TK if h == 0 else ["TTb"])

    def edges_again():
        cuts = [0, 256, 512, 768] + list(range(1024, 8193, 512))
        for j in range(len(cuts) - 1):
            a, b, k = cuts[j], cuts[j + 1], TURN[j % 6]
            mm(part(k, 0, b - a), T.C2[:], T.TT[:, a:b], True, True, ["C2"] + TK, bk(k))
            relu("av"[j % 2], a, b, k)

    def spread(y):
        k = (3, 1)[y % 2]
        buf = (T.E1, T.KS)[y % 2]
        for a in range(4 * y, 4 * y + 4):
            c0 = 512 * (y % 2) + 128 * (a % 4)
            for x in range(2):
                mm(buf[64 * x:64 * x + 64, c0:c0 + 128], T.SELI[32 * x:32 * x + 32, a, 0:64], T.DT[32 * x:32 * x + 32, :], True, True,
                   [("SELI", a), "DT"], bk(k))

    def spread_out(y):
        ramp("a", T.P2[:, 512 * y:512 * y + 512], (3, 1)[y % 2], [("P2", y)])

    for t in range(3):
        pi = t % 2
        if t == 0:
            edges_first()
        else:
            edges_again()

        def fetch(q):
            for e, a, b in (("v", 0, CUT[q]), ("a", CUT[q], 64)):
                cp(e, T.G[:, 1024 * q + 16 * a:1024 * q + 16 * b], T.R[:, 0:8192].indirect(T.IL[:, pi, 64 * q + a:64 * q + b]),
                   RK + [("IL", pi)], [("G", q, e)])

        def keys(q, term):
            if term == 0:
                mm(BANK[q][:, 0:256], T.ONE[0:1, :], T.KC[0:1, :], True, False, ["ONE", "KC"], bk(q))
            for c in range(8):
                o = BANK[q][:, 32 * c:32 * c + 32]
                if term == 1:
                    mm(o, T.G[:, 1024 * q + c:1024 * q + 1024:8], T.R1[:], False, c == 7, [("G", q, "v"), ("G", q, "a"), "R1"], bk(q))
                elif t < 2:
                    mm(o, T.P[0:64, 2048 * q + 2 * c + pi:2048 * q + 2048:16], T.R2[0:64, :], False, False, PK + R2K, bk(q))
                else:
                    a, x = 8 * (q % 2) + c, slice(64 * (q // 2), 64 * (q // 2) + 64)
                    mm(o, T.P2[x, 128 * a:128 * a + 128], T.R2[x, :], False, False, [("P2", a // 4)] + R2K, bk(q))

        def best(q):
            scan(T.SC[:, 256 * q:256 * q + 256], T.MSK[:], BANK[q][:, 0:256], A.add, A.min, ["MSK"], [("SC", q)] + bk(q))

        def aside(j):
            if t == 0 and j < 2:
                lists_mm(1, 6, j)
            if t == 1:
                steps_again(1, [j] if j < 2 else [2, 3])

        keys(0, 0); keys(1, 0)
        fetch(0); keys(0, 1); keys(2, 0); aside(0)
        fetch(1); keys(1, 1); keys(3, 0); aside(1); best(0)
        fetch(2); keys(2, 1); aside(2); best(1)
        mm(T.PM[:], T.OS[0:2, :], T.OM[0:2], True, False, ["OS", "OM"], bk(7))
        fetch(3); keys(3, 1); best(2)
        if t == 0:
            lists(1, 6)
            act(T.NID[:], T.IDN[:], F.Identity, ["IDN"], ["NID"], scale=-1.0)
            for x in range(2):
                for q in range(4):
                    dma("s", T.WL[32 * q:32 * q + 32, x, :], T.IL[0:32, x, 64 * q:64 * q + 64], "wl", [("IL", x)], [("WL", x, q)])
        X = T.E4[:, 0:24, 0:9]
        mm(X, T.ONE[0:1, :], T.ZR[0:1, 0:216], True, False, ["ONE", "ZR"], bk(6))
        best(3)
        if t == 0:
            steps_high(pi); steps_again(pi, range(4))
        else:
            if t == 1:
                spread(1); spread(0)
            cp("a", T.GW[:], T.WT[:].indirect(T.WL[:, pi, :]), WTK + ["WTb", "WTc"] + [("WL", pi, q) for q in range(4)], ["GW"])
            for c in range(8):
                mm(T.KS[:, c:64:8], T.GW[:, c::8], T.SW[:], True, True, ["GW", "SW"], bk(0))
            if t == 1:
                steps_low(pi)
            cp("a", T.WV[:], T.KS[:, 0:64], [], ["WV"] + bk(0))
            mm(T.E4[:, 16:24, 1:9], T.BD[:], T.WV[:], False, False, ["BD", "WV"], bk(6))
            mm(T.E4[:, 16:24, 0:8], T.NBD[:], T.WV[:], False, False, ["NBD", "WV"], bk(6))

        SCK = [("SC", q) for q in range(4)]
        key = T.SC[:, 15::16]
        ts(T.KR[:], key, R2048, -R2048, A.add, A.add, SCK, ["KR"])
        tt(T.FF[:], T.KR[:], key, A.is_gt, SCK + ["KR"], ["FF"])
        tt(T.ZZ[:], key, T.KR[:], A.subtract, SCK + ["KR"], ["ZZ"])
        for h in range(2):
            scan(T.LL[:, 32 * h:32 * h + 32], T.MK8[:], T.FF[:, h::2], A.mult, A.add, ["MK8", "FF"], [("LL", h)])
        LK = [("LL", 0), ("LL", 1)]
        nn = T.LL[:, 7::8]
        mm(T.E0[:, 0:8], T.TRI[:], nn, True, True, ["TRI"] + LK, bk(2))
        for c in range(8):
            mm(T.E4[:, 0:8, 1 + c], T.SH[:], nn, False, False, ["SH"] + LK, bk(6))
        ts(T.BB[:], T.ZZ[:], R32, -R32, A.add, A.add, ["ZZ"], ["BB"])
        for h in range(2):
            tt(T.TL[:, 32 * h:32 * h + 32], T.FF[:, h::2], T.LL[:, 32 * h:32 * h + 32], A.mult, ["FF", ("LL", h)], [("TL", h)])
            mm(T.E4[:, 8 + 4 * h:12 + 4 * h, 1:9], T.BD[:], T.BB[:, h::2], False, False, ["BD", "BB"], bk(6))
            mm(T.E4[:, 8 + 4 * h:12 + 4 * h, 0:8], T.NBD[:], T.BB[:, h::2], False, False, ["NBD", "BB"], bk(6))
        mm(T.E4[:, 0:8, 1:9], T.BD[:], T.TL[:], False, True, ["BD", ("TL", 0), ("TL", 1)], bk(6))
        if t == 0:
            steps_low(pi)
        cp("a", T.M1[:, pi, 0:3], X, [], [("M1d", pi)] + bk(6))
        for u in range(8):
            ts(T.U[:, u, :], T.IOTA[:], T.E0[:, u:u + 1], None, A.is_ge, None, ["IOTA"], [("U", u)] + bk(2))
        for us in (range(6), range(6, 8)):
            for u in us:
                mm(T.PM[:, 3:7, 9 * u:9 * u + 9], T.U[:, u, :], T.M2[:, pi, :, u, :], False, False, [("U", u), ("M2", pi, u % 4)], bk(7))
            for u in us:
                mm(T.PM[:, :, 9 * u:9 * u + 9], T.U[:, u, :], T.M1[:, pi, :, u, :], False, u == 7,
                   [("U", u), ("M1", pi, u % 4), ("M1d", pi)], bk(7))
        mm(T.E2[:, 0:64], T.IDN[:], T.LL[:], True, False, ["IDN"] + LK, bk(4))
        for h in range(2):
            mm(T.E2[:, 32 * h:32 * h + 32], T.D512[:], T.FF[:, h::2], False, False, ["D512", "FF"], bk(4))
        for c in range(8):
            mm(T.E2[:, c:64:8], T.TRI[:], nn, False, c == 7, ["TRI"] + LK, bk(4))
        for h in range(2):
            tt(T.OWN[:, 32 * h:32 * h + 32], T.ZZ[:, h::2], T.BB[:, h::2], A.subtract, ["ZZ", "BB"], [("OWN", h)])
            act(T.BST[:, 32 * h:32 * h + 32], T.BB[:, h::2], F.Identity, ["BB"], [("BST", h)], scale=1.0 / 32, bias=31.0)
        OK = [("OWN", 0), ("OWN", 1)]
        if t == 1:
            spread_out(1); spread_out(0)
        ts(T.NS[:], T.PM[:, 0, :], NEXT, None, A.not_equal, None, ["NEXT"], ["NS"] + bk(7))
        tt(T.DL[:], T.BST[:], T.OWN[:], A.subtract, [("BST", 0), ("BST", 1)] + OK, ["DL"])
        scan(T.SB[:, 9:81], T.NS[:], T.PM[:, 1, :], A.mult, A.add, ["NS"], ["SB"] + bk(7))
        if t > 0:
            scan(T.SB[:, 81:153], T.NS[:], T.PM[:, 2, :], A.mult, A.add, ["NS"], ["SBw"] + bk(7))
        mm(T.E0[0:17, 0:128], T.SB[:, 8:153:9], T.PERM[:], True, True, ["SB", "SBw", "PERM"], bk(2))
        cp("a", T.BT[0:17, :], T.E0[0:17, 0:128], [], ["BT"] + bk(2))
        for q in range(4):
            mm(T.E4[:, :, 4 * q:4 * q + 4], T.SELD[0:17, q, :], T.BT[0:17, :], True, True, [("SELD", q), "BT"], bk(6))
        ramp("a", T.DS[:], 6, ["DS"])
        for i in range(4):
            scan(T.SI[:, 72 * i:72 * i + 72], T.NS[:], T.PM[:, 3 + i, :], A.mult, A.add, ["NS"], [("SI", i)] + bk(7))
        ts(T.GO[:], T.E2[:, 0:64], -383.5, None, A.is_lt, None, [], ["GO"] + bk(4))
        for x in range(4):
            scaled("v", T.ST[:, x::4], T.SI[:, 8::9], T.MZ[:, x:x + 1], [("SI", i) for i in range(4)] + ["MZ"], [("ST", x)])
        mm(T.E1[:, 0:32], T.ST[:], T.EI[:], True, True, [("ST", x) for x in range(4)] + ["EI"], bk(3))
        tt(T.GD[:], T.GO[:], T.DL[:], A.mult, ["GO", "DL"], ["GD"])
        cp("v", T.OFF[:], T.E1[:, 0:32], [], ["OFF"] + bk(3))
        mm(T.E2[:, 0:64], T.IDN[:], T.OWN[:], True, False, OK + ["IDN"], bk(4))
        mm(T.E2[:, 0:64], T.IDN[:], T.GD[:], False, True, ["GD", "IDN"], bk(4))
        for h in range(2):
            if t == 0:
                cp("a", T.NB[:, :, h, :], T.E2[:, 32 * h:32 * h + 32], [], [("NB", h)] + bk(4))
            else:
                cp("a", T.NPO[:, :, h, pi::2], T.E2[:, 32 * h:32 * h + 32], [], [("NPO", pi, h)] + bk(4))
        if t == 0:
            steps_mm(1, range(4))
            mm(BANK[1][:, 0:128], T.DNZ[:], T.C[:], True, False, ["DNZ"] + CK, bk(1))
            for s_ in range(2):
                mm(BANK[1][:, 0:128], T.RS[0:4, s_, :], T.SP[0:4, s_], False, s_ == 1, [("RS", s_), ("SP", s_)], bk(1))
            mm(T.E0[0:64, 0:128], T.NB[:], T.IDN[:], True, True, [("NB", 0), ("NB", 1), "IDN"], bk(2))
            cp("a", T.C2[:], BANK[1][:, 0:128], [], ["C2"] + bk(1))
            cp("a", T.DT[0:64, :], T.E0[0:64, 0:128], [], ["DT"] + bk(2))
        if t == 0:
            tt(T.DG[:], T.WT[:].indirect(T.OFF[:]), T.DS[:], A.mult, WTK + ["WTb", "OFF", "DS"], ["DG"])
            cp("v", T.TT[:].indirect(T.OFF[:]), T.DG[:], ["DG", "OFF"], TK + ["TTb"])
            for x in range(2, 8):
                dma("s", T.WT[16 * x + 15:16 * x + 16, 0:8192], T.W[x % 2:8:2, :], "w4", WK, WTK if x == 2 else ["WTc"] if x == 7 else [])
            steps_high(1)
        else:
            cp("v", T.TT[:].indirect(T.OFF[:]), T.DS[:], ["DS", "OFF"], TK)
        if t == 1:
            spread(3); spread(2); spread_out(3); spread_out(2)
        if t == 2:
            mm(BANK[1][:, 0:32], T.DNZ[:], T.Z[:], True, False, ["DNZ", "Z"], bk(1))
            for s_ in range(2):
                mm(BANK[1][:, 0:32], T.RS[0:4, s_, :], T.SP[0:4, s_, 2:4], False, s_ == 1, [("RS", s_), ("SP", s_)], bk(1))
            for h in range(2):
                cp("a", T.CC[:, :, h], BANK[1][:, 16 * h:16 * h + 16], [], [("CC", h)] + bk(1))
            act(T.Yj[mine], T.Yw[mine], F.Identity, [("Yw", q) for q in range(4)], ["Yj", ("ACC", 10)],
                accum_out=T.ACC[mine, 10:11])
            scaled("a", T.MW[:], T.HM[:, 0:32:16], 15.0, ["HM"], ["MW"])

    NK = [("NPO", pi, h) for pi in range(2) for h in range(2)]
    fused(1, "oa", lambda b: T.NPO[:, b], T.LO[:, me], NK)
    for b in order:
        for h in range(2):
            src, keys_ = (T.NPO[:, me, h, :], NK) if b == me else (T.LO[:, b, h, :], [("LO", b)])
            dma("s", T.newpart[2 * b + h:2 * b + h + 1, :], src, "dn", keys_, [])

    cutp = T.E3[0:1, 0:2]
    mm(cutp, T.ACC[mine, 10:11], T.MW[mine, :], True, False, [("ACC", 10), "MW"], bk(5))
    a0 = 0
    for k, (m, who) in enumerate(PIECES):
        for a in range(m):
            c0 = 128 * (a0 + a)
            mm(BANK[k][:, 32 * a:32 * a + 32], T.TT[:, c0:c0 + 128], T.CC[:], True, True, TK + [("CC", 0), ("CC", 1)], bk(k))
        a0 += m
        for h in range(2):
            j = 2 * k + h
            junk = T.R[:, 512 * j:512 * j + 16 * m]
            if who[h] == "v":
                ts(junk, BANK[k][:, h:32 * m:2], 0.0, None, A.max, None, [], [("R", j)] + bk(k))
            else:
                act(junk, BANK[k][:, h:32 * m:2], F.Relu, [], [("R", j), ("ACC", j)] + bk(k), accum_out=T.ACC[:, j:j + 1])
        for h in range(2):
            j = 2 * k + h
            if who[h] == "v":
                op("v", lambda: V.tensor_reduce(T.ACC[:, j:j + 1], T.R[:, 512 * j:512 * j + 16 * m], AX.X, A.add), [("R", j)], [("ACC", j)])
    for k in range(len(PIECES)):
        mm(cutp, T.NG[:], T.ACC[:, 2 * k:2 * k + 2], False, k == len(PIECES) - 1, [("ACC", 2 * k), ("ACC", 2 * k + 1), "NG"], bk(5))
    cp("v", T.CL[0:1, me, 0:2], cutp, [], ["CLown"] + bk(5))
    to_all(T.sem.ca, T.CL[:, me, :], ["CLown"])
    dma("a", T.cut[:], T.CL[0:1, :, 0:2], "dc", ["CLown", "CLfar"], [])

    for s in SEMAPHORES:
        if cnt[s] > waited[s]:
            (g if s in ("sent", "eg") else g.sync).wait_ge(T.sem[s], cnt[s])
